import numpy as np
import ml_dtypes


def mxq(x, axis, fmt="e4m3"):
    dtype, down = {"e4m3": (ml_dtypes.float8_e4m3fn, 7), "e5m2": (ml_dtypes.float8_e5m2, 14)}[fmt]
    v = np.moveaxis(np.asarray(x, np.float32).astype(ml_dtypes.bfloat16).astype(np.float64), axis, -1)
    blocks = v.reshape(v.shape[:-1] + (-1, 32))
    amax = np.abs(blocks).max(-1, keepdims=True)
    byte = np.maximum(np.where(amax > 0, np.frexp(amax)[1] - 1 + 127, 0) - down, 1)
    scale = np.exp2(byte - 127.0)
    codes = (blocks / scale).astype(np.float32).astype(dtype).astype(np.float64)
    return np.moveaxis((codes * scale).reshape(v.shape), -1, axis)


WIDE = False


def mx_kscale(k, group=512):
    if not WIDE:
        return np.ones(k)
    levels = np.array([10, -10, 5, -5, 0])
    if group != 512:
        return np.exp2(np.random.permutation(np.resize(levels, k // group))).repeat(group)
    if k % 512:
        return np.exp2(np.random.permutation(np.resize(levels, k // 32))).repeat(32)
    a = np.empty((k // 512, 16))
    for p in range(k // 512):
        a[p, :8] = np.random.permutation(np.resize(levels, 8))
        for g in range(8):
            far = levels[np.abs(levels - a[p, g]) >= 10]
            a[p, g + 8] = far[np.random.randint(len(far))]
    return np.exp2(a.ravel()).repeat(32)


def f64(x):
    return np.asarray(x).astype(np.float64)


G, D, M, N = 2, 256, 128, 512


def setup_inputs():
    n = np.random.standard_normal
    s = mx_kscale(D, 0)[:, None]
    return {
        "x": (n((G, D, N)) * s).astype(np.float32),
        "w": (n((G, D, M)) / np.sqrt(D) / s).astype(np.float32),
        "u": (n((G, D, M)) / np.sqrt(D) / s).astype(np.float32),
    }


def reference(x, w, u):
    xq = mxq(f64(x), 1, "e4m3")
    h = mxq(f64(w), 1, "e4m3").transpose(0, 2, 1) @ xq
    g = mxq(f64(u), 1, "e4m3").transpose(0, 2, 1) @ xq
    y = np.tanh(h) * g
    return y

@@ -1,0 +1,148 @@
+from contextlib import ExitStack
+
+import concourse.mybir as mybir
+
+G, D, M, N = 2, 256, 128, 512
+FLOPS = 2 * 2 * G * D * M * N
+
+F32 = mybir.dt.float32
+BF16 = mybir.dt.bfloat16
+U32 = mybir.dt.uint32
+U8 = mybir.dt.uint8
+FP8X4 = mybir.dt.float8_e4m3fn_x4
+TANH = mybir.ActivationFunctionType.Tanh
+MULT = mybir.AluOpType.mult
+
+P = 128
+PACK = 4
+ROWS = D // PACK
+NT = 128
+PAIR = 2
+
+
+def tile_rows_gglu_tanh_kernel(tc, x, w, u, out):
+    nc = tc.nc
+    x_rows = x.rearrange("g d n -> (g d) n").rearrange("(p j) n -> p j n", j=PACK)
+    w_rows = w.rearrange("g d m -> (g d) m").rearrange("(p j) m -> p j m", j=PACK)
+    u_rows = u.rearrange("g d m -> (g d) m").rearrange("(p j) m -> p j m", j=PACK)
+    chunks = [(0, 256), (256, 128), (384, 128)]
+
+    with ExitStack() as ctx:
+        sb = ctx.enter_context(tc.tile_pool(name="sb", bufs=1))
+        ps = ctx.enter_context(tc.psum_pool(name="ps", bufs=1))
+        ctx.enter_context(tc.manual_schedule())
+
+        def operand(name, width):
+            return {
+                "raw": sb.tile([P, PACK, width], F32, name=name + "_raw", align_bytes=64),
+                "packed": sb.tile([P, width, PACK], BF16, name=name + "_packed", align_bytes=64),
+                "codes": sb.tile([P, width], U32, name=name + "_codes", align_bytes=64),
+                "scales": sb.tile([P, width], U8, name=name + "_scales", align_bytes=64),
+            }
+
+        wq = operand("w", M)
+        uq = operand("u", M)
+        xq = [operand("x%d" % i, width) for i, (first, width) in enumerate(chunks)]
+        banks = [[ps.tile([P, 512], F32, name="bank%d_%d" % (g, b)) for b in range(4)] for g in range(G)]
+        act = [[sb.tile([P, width], F32, name="act%d_%d" % (i, g)) for g in range(G)] for i, (first, width) in enumerate(chunks)]
+        res = [sb.tile([P, G, width], F32, name="res%d" % i) for i, (first, width) in enumerate(chunks)]
+        h_at = [(0, 0), (2, 0), (0, 256)]
+        g_at = [(1, 0), (2, 128), (3, 0)]
+
+        def interleave(engine, op, lo, hi):
+            dst = op["packed"][:, lo:hi, :].rearrange("p (c i) j -> p c j i", i=PAIR)
+            src = op["raw"][:, :, lo:hi].rearrange("p j (c i) -> p c j i", i=PAIR)
+            if engine == "vector":
+                nc.vector.tensor_copy(out=dst, in_=src)
+            else:
+                nc.scalar.copy(out=dst, in_=src)
+
+        def quantize(op, lo, hi):
+            nc.vector.quantize_mx(
+                out=op["codes"][:, lo:hi].bitcast(FP8X4),
+                scales=op["scales"][:, lo:hi],
+                in_=op["packed"][:, lo:hi, :].rearrange("p c j -> p (c j)"),
+            )
+
+        def multiply(weights, place, i, lo):
+            bank, first = place[i]
+            for g in range(G):
+                rows = slice(ROWS * g, ROWS * (g + 1))
+                nc.tensor.matmul_mx(
+                    out=banks[g][bank][:, first + lo : first + lo + NT],
+                    lhsT=weights["codes"][rows, :].bitcast(FP8X4),
+                    lhsT_scale=weights["scales"][rows, :],
+                    rhs=xq[i]["codes"][rows, lo : lo + NT].bitcast(FP8X4),
+                    rhs_scale=xq[i]["scales"][rows, lo : lo + NT],
+                    start=True,
+                    stop=True,
+                )
+
+        def tanh(i, g):
+            bank, first = h_at[i]
+            nc.scalar.activation(out=act[i][g][:], in_=banks[g][bank][:, first : first + chunks[i][1]], func=TANH)
+
+        def gate(i, g):
+            bank, first = g_at[i]
+            nc.vector.tensor_tensor(
+                out=res[i][:, g, :], in0=banks[g][bank][:, first : first + chunks[i][1]], in1=act[i][g][:], op=MULT
+            )
+
+        def store(i, g):
+            first, width = chunks[i]
+            nc.sync.dma_start(out=out[g, :, first : first + width], in_=res[i][:, g, :])
+
+        def load_x(i):
+            first, width = chunks[i]
+            nc.sync.dma_start(out=xq[i]["raw"][:], in_=x_rows[:, :, first : first + width])
+
+        nc.sync.dma_start(out=wq["raw"][:], in_=w_rows)
+        load_x(0)
+        nc.sync.dma_start(out=uq["raw"][:], in_=u_rows)
+        load_x(1)
+        load_x(2)
+
+        warm = sb.tile([P, 8], F32, name="warm")
+        warm_out = sb.tile([P, 8], F32, name="warm_out")
+        nc.vector.memset(warm[:], 0.0)
+        nc.scalar.activation(out=warm_out[:], in_=warm[:], func=TANH)
+
+        interleave("vector", wq, 0, M)
+        quantize(wq, 0, M)
+
+        interleave("vector", xq[0], 0, 128)
+        interleave("scalar", xq[0], 128, 208)
+        interleave("vector", xq[0], 208, 256)
+        quantize(xq[0], 0, 128)
+        multiply(wq, h_at, 0, 0)
+        quantize(xq[0], 128, 256)
+        multiply(wq, h_at, 0, 128)
+        interleave("scalar", uq, 0, M)
+        quantize(uq, 0, M)
+        multiply(uq, g_at, 0, 0)
+        multiply(uq, g_at, 0, 128)
+        tanh(0, 0)
+        tanh(0, 1)
+
+        interleave("vector", xq[1], 0, 128)
+        quantize(xq[1], 0, 128)
+        multiply(wq, h_at, 1, 0)
+        multiply(uq, g_at, 1, 0)
+
+        interleave("vector", xq[2], 0, 64)
+        interleave("scalar", xq[2], 64, 128)
+        gate(0, 0)
+        store(0, 0)
+        quantize(xq[2], 0, 128)
+        multiply(wq, h_at, 2, 0)
+        multiply(uq, g_at, 2, 0)
+        gate(0, 1)
+        store(0, 1)
+        for g in range(G):
+            tanh(1, g)
+            gate(1, g)
+        nc.sync.dma_start(out=out[:, :, 256:384].rearrange("g m n -> m g n"), in_=res[1][:])
+        for g in range(G):
+            tanh(2, g)
+            gate(2, g)
+            store(2, g)

@@ -18,131 +18,138 @@ PACK = 4
 ROWS = D // PACK
 NT = 128
 PAIR = 2
+COPY = mybir.ActivationFunctionType.Copy
 
 
 def tile_rows_gglu_tanh_kernel(tc, x, w, u, out):
     nc = tc.nc
-    x_rows = x.rearrange("g d n -> (g d) n").rearrange("(p j) n -> p j n", j=PACK)
+    x_pairs = x.rearrange("g d n -> (g d) n").rearrange("(p h e) n -> p h (e n)", h=2, e=2)
     w_rows = w.rearrange("g d m -> (g d) m").rearrange("(p j) m -> p j m", j=PACK)
     u_rows = u.rearrange("g d m -> (g d) m").rearrange("(p j) m -> p j m", j=PACK)
-    chunks = [(0, 256), (256, 128), (384, 128)]
 
     with ExitStack() as ctx:
         sb = ctx.enter_context(tc.tile_pool(name="sb", bufs=1))
         ps = ctx.enter_context(tc.psum_pool(name="ps", bufs=1))
         ctx.enter_context(tc.manual_schedule())
 
-        def operand(name, width):
+        def operand(name, raw, width):
             return {
-                "raw": sb.tile([P, PACK, width], F32, name=name + "_raw", align_bytes=64),
+                "raw": raw,
                 "packed": sb.tile([P, width, PACK], BF16, name=name + "_packed", align_bytes=64),
                 "codes": sb.tile([P, width], U32, name=name + "_codes", align_bytes=64),
                 "scales": sb.tile([P, width], U8, name=name + "_scales", align_bytes=64),
             }
 
-        wq = operand("w", M)
-        uq = operand("u", M)
-        xq = [operand("x%d" % i, width) for i, (first, width) in enumerate(chunks)]
+        w_raw = sb.tile([P, PACK, M], F32, name="w_raw", align_bytes=64)
+        u_raw = sb.tile([P, PACK, M], F32, name="u_raw", align_bytes=64)
+        x_raw = sb.tile([P, 2, 2 * N], F32, name="x_raw", align_bytes=64)
+        wq = operand("w", w_raw[:], M)
+        uq = operand("u", u_raw[:], M)
+        xq = operand("x", x_raw[:].rearrange("p h (e n) -> p (h e) n", e=2), N)
         banks = [[ps.tile([P, 512], F32, name="bank%d_%d" % (g, b)) for b in range(4)] for g in range(G)]
-        act = [[sb.tile([P, width], F32, name="act%d_%d" % (i, g)) for g in range(G)] for i, (first, width) in enumerate(chunks)]
-        res = [sb.tile([P, G, width], F32, name="res%d" % i) for i, (first, width) in enumerate(chunks)]
-        h_at = [(0, 0), (2, 0), (0, 256)]
-        g_at = [(1, 0), (2, 128), (3, 0)]
+        act = [sb.tile([P, N], F32, name="act%d" % g) for g in range(G)]
+        res = [sb.tile([P, N], F32, name="res%d" % g) for g in range(G)]
+        h_at = [[(0, 0), (0, 128), (2, 0), (0, 256)]] * 2
+        g_at = [[(1, 0), (1, 128), (3, 0), (1, 256)]] * 2
 
-        def interleave(engine, op, lo, hi):
+        def views(op, lo, hi):
             dst = op["packed"][:, lo:hi, :].rearrange("p (c i) j -> p c j i", i=PAIR)
             src = op["raw"][:, :, lo:hi].rearrange("p j (c i) -> p c j i", i=PAIR)
-            if engine == "vector":
-                nc.vector.tensor_copy(out=dst, in_=src)
-            else:
-                nc.scalar.copy(out=dst, in_=src)
+            return dst, src
 
-        def quantize(op, lo, hi):
+        def pack_v(op, lo, hi):
+            dst, src = views(op, lo, hi)
+            nc.vector.tensor_copy(out=dst, in_=src)
+
+        def pack_s(op, lo, hi):
+            dst, src = views(op, lo, hi)
+            nc.scalar.copy(out=dst, in_=src)
+
+        def pack_a(op, lo, hi):
+            dst, src = views(op, lo, hi)
+            nc.scalar.activation(out=dst, in_=src, func=COPY)
+
+        def quantize(op, b):
+            lo, hi = NT * b, NT * (b + 1)
             nc.vector.quantize_mx(
                 out=op["codes"][:, lo:hi].bitcast(FP8X4),
                 scales=op["scales"][:, lo:hi],
                 in_=op["packed"][:, lo:hi, :].rearrange("p c j -> p (c j)"),
             )
 
-        def multiply(weights, place, i, lo):
-            bank, first = place[i]
-            for g in range(G):
+        def multiply(weights, place, b, groups=(0, 1)):
+            cols = slice(NT * b, NT * (b + 1))
+            for g in groups:
+                bank, first = place[g][b]
                 rows = slice(ROWS * g, ROWS * (g + 1))
                 nc.tensor.matmul_mx(
-                    out=banks[g][bank][:, first + lo : first + lo + NT],
+                    out=banks[g][bank][:, first : first + NT],
                     lhsT=weights["codes"][rows, :].bitcast(FP8X4),
                     lhsT_scale=weights["scales"][rows, :],
-                    rhs=xq[i]["codes"][rows, lo : lo + NT].bitcast(FP8X4),
-                    rhs_scale=xq[i]["scales"][rows, lo : lo + NT],
+                    rhs=xq["codes"][rows, cols].bitcast(FP8X4),
+                    rhs_scale=xq["scales"][rows, cols],
                     start=True,
                     stop=True,
                 )
 
-        def tanh(i, g):
-            bank, first = h_at[i]
-            nc.scalar.activation(out=act[i][g][:], in_=banks[g][bank][:, first : first + chunks[i][1]], func=TANH)
-
-        def gate(i, g):
-            bank, first = g_at[i]
-            nc.vector.tensor_tensor(
-                out=res[i][:, g, :], in0=banks[g][bank][:, first : first + chunks[i][1]], in1=act[i][g][:], op=MULT
+        def tanh(g, b, count):
+            bank, first = h_at[g][b]
+            nc.scalar.activation(
+                out=act[g][:, NT * b : NT * (b + count)], in_=banks[g][bank][:, first : first + NT * count], func=TANH
             )
 
-        def store(i, g):
-            first, width = chunks[i]
-            nc.sync.dma_start(out=out[g, :, first : first + width], in_=res[i][:, g, :])
+        def gate(g, b, count):
+            bank, first = g_at[g][b]
+            cols = slice(NT * b, NT * (b + count))
+            nc.vector.tensor_tensor(
+                out=res[g][:, cols], in0=banks[g][bank][:, first : first + NT * count], in1=act[g][:, cols], op=MULT
+            )
 
-        def load_x(i):
-            first, width = chunks[i]
-            nc.sync.dma_start(out=xq[i]["raw"][:], in_=x_rows[:, :, first : first + width])
+        def store(g, b, count, eng=None):
+            cols = slice(NT * b, NT * (b + count))
+            (eng or nc.sync).dma_start(out=out[g, :, cols], in_=res[g][:, cols])
 
-        nc.sync.dma_start(out=wq["raw"][:], in_=w_rows)
-        load_x(0)
-        nc.sync.dma_start(out=uq["raw"][:], in_=u_rows)
-        load_x(1)
-        load_x(2)
+        def load_x(lo, hi):
+            nc.sync.dma_start(out=x_raw[:, :, lo:hi], in_=x_pairs[:, :, lo:hi])
 
-        warm = sb.tile([P, 8], F32, name="warm")
-        warm_out = sb.tile([P, 8], F32, name="warm_out")
-        nc.vector.memset(warm[:], 0.0)
-        nc.scalar.activation(out=warm_out[:], in_=warm[:], func=TANH)
-
-        interleave("vector", wq, 0, M)
-        quantize(wq, 0, M)
-
-        interleave("vector", xq[0], 0, 128)
-        interleave("scalar", xq[0], 128, 208)
-        interleave("vector", xq[0], 208, 256)
-        quantize(xq[0], 0, 128)
-        multiply(wq, h_at, 0, 0)
-        quantize(xq[0], 128, 256)
-        multiply(wq, h_at, 0, 128)
-        interleave("scalar", uq, 0, M)
-        quantize(uq, 0, M)
-        multiply(uq, g_at, 0, 0)
-        multiply(uq, g_at, 0, 128)
-        tanh(0, 0)
-        tanh(0, 1)
-
-        interleave("vector", xq[1], 0, 128)
-        quantize(xq[1], 0, 128)
-        multiply(wq, h_at, 1, 0)
-        multiply(uq, g_at, 1, 0)
-
-        interleave("vector", xq[2], 0, 64)
-        interleave("scalar", xq[2], 64, 128)
-        gate(0, 0)
-        store(0, 0)
-        quantize(xq[2], 0, 128)
-        multiply(wq, h_at, 2, 0)
-        multiply(uq, g_at, 2, 0)
-        gate(0, 1)
-        store(0, 1)
-        for g in range(G):
-            tanh(1, g)
-            gate(1, g)
-        nc.sync.dma_start(out=out[:, :, 256:384].rearrange("g m n -> m g n"), in_=res[1][:])
-        for g in range(G):
-            tanh(2, g)
-            gate(2, g)
-            store(2, g)
+        nc.sync.dma_start(out=w_raw[:], in_=w_rows)
+        load_x(0, N + 256)
+        nc.sync.dma_start(out=u_raw[:], in_=u_rows)
+        load_x(N + 256, N + 384)
+        load_x(N + 384, N + 512)
+        pack_v(wq, 0, 80)
+        pack_a(wq, 80, 128)
+        quantize(wq, 0)
+        pack_v(xq, 0, 80)
+        pack_s(xq, 80, 128)
+        pack_v(xq, 128, 256)
+        quantize(xq, 0)
+        multiply(wq, h_at, 0)
+        pack_v(uq, 0, 64)
+        pack_s(uq, 64, 128)
+        quantize(xq, 1)
+        multiply(wq, h_at, 1)
+        pack_v(xq, 256, 304)
+        pack_s(xq, 304, 384)
+        quantize(uq, 0)
+        multiply(uq, g_at, 0)
+        multiply(uq, g_at, 1)
+        pack_v(xq, 384, 480)
+        pack_s(xq, 480, 512)
+        quantize(xq, 2)
+        multiply(wq, h_at, 2)
+        multiply(uq, g_at, 2)
+        quantize(xq, 3)
+        tanh(0, 0, 2)
+        tanh(1, 0, 2)
+        gate(0, 0, 2)
+        store(0, 0, 2)
+        gate(1, 0, 2)
+        store(1, 0, 2)
+        multiply(wq, h_at, 3)
+        multiply(uq, g_at, 3)
+        for b in (2, 3):
+            for g in range(G):
+                tanh(g, b, 1)
+                gate(g, b, 1)
+                store(g, b, 1)

@@ -46,11 +46,11 @@ def tile_rows_gglu_tanh_kernel(tc, x, w, u, out):
         wq = operand("w", w_raw[:], M)
         uq = operand("u", u_raw[:], M)
         xq = operand("x", x_raw[:].rearrange("p h (e n) -> p (h e) n", e=2), N)
-        banks = [[ps.tile([P, 512], F32, name="bank%d_%d" % (g, b)) for b in range(4)] for g in range(G)]
+        banks = [[ps.tile([P, 512], F32, name="bank%d_%d" % (g, b)) for b in range(4 - g)] for g in range(G)]
         act = [sb.tile([P, N], F32, name="act%d" % g) for g in range(G)]
         res = [sb.tile([P, N], F32, name="res%d" % g) for g in range(G)]
         h_at = [[(0, 0), (0, 128), (2, 0), (0, 256)]] * 2
-        g_at = [[(1, 0), (1, 128), (3, 0), (1, 256)]] * 2
+        g_at = [[(1, 0), (1, 128), (3, 0), (1, 256)], [(1, 0), (1, 128), (2, 128), (1, 256)]]
 
         def views(op, lo, hi):
             dst = op["packed"][:, lo:hi, :].rearrange("p (c i) j -> p c j i", i=PAIR)
@@ -112,6 +112,7 @@ def tile_rows_gglu_tanh_kernel(tc, x, w, u, out):
         def load_x(lo, hi):
             nc.sync.dma_start(out=x_raw[:, :, lo:hi], in_=x_pairs[:, :, lo:hi])
 
+        spare = ps.tile([P, 512], F32, name="spare")
         nc.sync.dma_start(out=w_raw[:], in_=w_rows)
         load_x(0, N + 256)
         nc.sync.dma_start(out=u_raw[:], in_=u_rows)
@@ -120,6 +121,8 @@ def tile_rows_gglu_tanh_kernel(tc, x, w, u, out):
         pack_v(wq, 0, 80)
         pack_a(wq, 80, 128)
         quantize(wq, 0)
+        for i in range(11):
+            nc.tensor.matmul_mx(out=spare[:, NT * (i % 4) : NT * (i % 4 + 1)], lhsT=wq["codes"][:].bitcast(FP8X4), lhsT_scale=wq["scales"][:], rhs=wq["codes"][:].bitcast(FP8X4), rhs_scale=wq["scales"][:], start=True, stop=True)
         pack_v(xq, 0, 80)
         pack_s(xq, 80, 128)
         pack_v(xq, 128, 256)

@@ -11,6 +11,7 @@ U32 = mybir.dt.uint32
 U8 = mybir.dt.uint8
 FP8X4 = mybir.dt.float8_e4m3fn_x4
 TANH = mybir.ActivationFunctionType.Tanh
+COPY = mybir.ActivationFunctionType.Copy
 MULT = mybir.AluOpType.mult
 
 P = 128
@@ -18,12 +19,12 @@ PACK = 4
 ROWS = D // PACK
 NT = 128
 PAIR = 2
-COPY = mybir.ActivationFunctionType.Copy
 
 
 def tile_rows_gglu_tanh_kernel(tc, x, w, u, out):
     nc = tc.nc
     x_pairs = x.rearrange("g d n -> (g d) n").rearrange("(p h e) n -> p h (e n)", h=2, e=2)
+    x_rows = x.rearrange("g d n -> (g d) n").rearrange("(p j) n -> p j n", j=PACK)
     w_rows = w.rearrange("g d m -> (g d) m").rearrange("(p j) m -> p j m", j=PACK)
     u_rows = u.rearrange("g d m -> (g d) m").rearrange("(p j) m -> p j m", j=PACK)
 
@@ -43,14 +44,15 @@ def tile_rows_gglu_tanh_kernel(tc, x, w, u, out):
         w_raw = sb.tile([P, PACK, M], F32, name="w_raw", align_bytes=64)
         u_raw = sb.tile([P, PACK, M], F32, name="u_raw", align_bytes=64)
         x_raw = sb.tile([P, 2, 2 * N], F32, name="x_raw", align_bytes=64)
+        x_four = x_raw[:].rearrange("p h (e n) -> p (h e) n", e=2)
         wq = operand("w", w_raw[:], M)
         uq = operand("u", u_raw[:], M)
-        xq = operand("x", x_raw[:].rearrange("p h (e n) -> p (h e) n", e=2), N)
-        banks = [[ps.tile([P, 512], F32, name="bank%d_%d" % (g, b)) for b in range(4 - g)] for g in range(G)]
+        xq = operand("x", x_four, N)
+        banks = [[ps.tile([P, 512], F32, name="bank%d_%d" % (g, b)) for b in range(4)] for g in range(G)]
         act = [sb.tile([P, N], F32, name="act%d" % g) for g in range(G)]
         res = [sb.tile([P, N], F32, name="res%d" % g) for g in range(G)]
-        h_at = [[(0, 0), (0, 128), (2, 0), (0, 256)]] * 2
-        g_at = [[(1, 0), (1, 128), (3, 0), (1, 256)], [(1, 0), (1, 128), (2, 128), (1, 256)]]
+        h_at = [(0, 0), (0, 128), (2, 0), (3, 0)]
+        g_at = [(1, 0), (1, 128), (0, 256), (2, 128)]
 
         def views(op, lo, hi):
             dst = op["packed"][:, lo:hi, :].rearrange("p (c i) j -> p c j i", i=PAIR)
@@ -69,8 +71,8 @@ def tile_rows_gglu_tanh_kernel(tc, x, w, u, out):
             dst, src = views(op, lo, hi)
             nc.scalar.activation(out=dst, in_=src, func=COPY)
 
-        def quantize(op, b):
-            lo, hi = NT * b, NT * (b + 1)
+        def quantize(op, b, count=1):
+            lo, hi = NT * b, NT * (b + count)
             nc.vector.quantize_mx(
                 out=op["codes"][:, lo:hi].bitcast(FP8X4),
                 scales=op["scales"][:, lo:hi],
@@ -79,8 +81,8 @@ def tile_rows_gglu_tanh_kernel(tc, x, w, u, out):
 
         def multiply(weights, place, b, groups=(0, 1)):
             cols = slice(NT * b, NT * (b + 1))
+            bank, first = place[b]
             for g in groups:
-                bank, first = place[g][b]
                 rows = slice(ROWS * g, ROWS * (g + 1))
                 nc.tensor.matmul_mx(
                     out=banks[g][bank][:, first : first + NT],
@@ -93,13 +95,13 @@ def tile_rows_gglu_tanh_kernel(tc, x, w, u, out):
                 )
 
         def tanh(g, b, count):
-            bank, first = h_at[g][b]
+            bank, first = h_at[b]
             nc.scalar.activation(
                 out=act[g][:, NT * b : NT * (b + count)], in_=banks[g][bank][:, first : first + NT * count], func=TANH
             )
 
         def gate(g, b, count):
-            bank, first = g_at[g][b]
+            bank, first = g_at[b]
             cols = slice(NT * b, NT * (b + count))
             nc.vector.tensor_tensor(
                 out=res[g][:, cols], in0=banks[g][bank][:, first : first + NT * count], in1=act[g][:, cols], op=MULT
@@ -112,47 +114,47 @@ def tile_rows_gglu_tanh_kernel(tc, x, w, u, out):
         def load_x(lo, hi):
             nc.sync.dma_start(out=x_raw[:, :, lo:hi], in_=x_pairs[:, :, lo:hi])
 
-        spare = ps.tile([P, 512], F32, name="spare")
-        nc.sync.dma_start(out=w_raw[:], in_=w_rows)
+        def load_cols(lo, hi):
+            nc.sync.dma_start(out=x_four[:, :, lo:hi], in_=x_rows[:, :, lo:hi])
+
         load_x(0, N + 256)
+        nc.sync.dma_start(out=w_raw[:], in_=w_rows)
         nc.sync.dma_start(out=u_raw[:], in_=u_rows)
         load_x(N + 256, N + 384)
         load_x(N + 384, N + 512)
+        pack_v(xq, 0, 192)
+        pack_a(xq, 192, 256)
         pack_v(wq, 0, 80)
-        pack_a(wq, 80, 128)
+        pack_s(wq, 80, 128)
+        quantize(xq, 0, 2)
         quantize(wq, 0)
-        for i in range(11):
-            nc.tensor.matmul_mx(out=spare[:, NT * (i % 4) : NT * (i % 4 + 1)], lhsT=wq["codes"][:].bitcast(FP8X4), lhsT_scale=wq["scales"][:], rhs=wq["codes"][:].bitcast(FP8X4), rhs_scale=wq["scales"][:], start=True, stop=True)
-        pack_v(xq, 0, 80)
-        pack_s(xq, 80, 128)
-        pack_v(xq, 128, 256)
-        quantize(xq, 0)
         multiply(wq, h_at, 0)
-        pack_v(uq, 0, 64)
-        pack_s(uq, 64, 128)
-        quantize(xq, 1)
         multiply(wq, h_at, 1)
-        pack_v(xq, 256, 304)
-        pack_s(xq, 304, 384)
+        pack_v(uq, 0, 80)
+        pack_s(uq, 80, 128)
+        pack_v(xq, 256, 336)
+        pack_s(xq, 336, 384)
         quantize(uq, 0)
         multiply(uq, g_at, 0)
         multiply(uq, g_at, 1)
-        pack_v(xq, 384, 480)
-        pack_s(xq, 480, 512)
+        pack_v(xq, 384, 464)
+        pack_s(xq, 464, 512)
         quantize(xq, 2)
         multiply(wq, h_at, 2)
-        multiply(uq, g_at, 2)
         quantize(xq, 3)
-        tanh(0, 0, 2)
-        tanh(1, 0, 2)
-        gate(0, 0, 2)
-        store(0, 0, 2)
-        gate(1, 0, 2)
-        store(1, 0, 2)
         multiply(wq, h_at, 3)
+        for g in range(G):
+            tanh(g, 0, 2)
+        multiply(uq, g_at, 2)
+        for g in range(G):
+            gate(g, 0, 2)
+            store(g, 0, 2)
+        for g in range(G):
+            tanh(g, 2, 1)
         multiply(uq, g_at, 3)
+        for g in range(G):
+            tanh(g, 3, 1)
         for b in (2, 3):
             for g in range(G):
-                tanh(g, b, 1)
                 gate(g, b, 1)
                 store(g, b, 1)

@@ -117,11 +117,11 @@ def tile_rows_gglu_tanh_kernel(tc, x, w, u, out):
         def load_cols(lo, hi):
             nc.sync.dma_start(out=x_four[:, :, lo:hi], in_=x_rows[:, :, lo:hi])
 
-        load_x(0, N + 256)
+        load_cols(0, 256)
         nc.sync.dma_start(out=w_raw[:], in_=w_rows)
         nc.sync.dma_start(out=u_raw[:], in_=u_rows)
-        load_x(N + 256, N + 384)
-        load_x(N + 384, N + 512)
+        load_cols(256, 384)
+        load_cols(384, 512)
         pack_v(xq, 0, 192)
         pack_a(xq, 192, 256)
         pack_v(wq, 0, 80)
@@ -141,11 +141,11 @@ def tile_rows_gglu_tanh_kernel(tc, x, w, u, out):
         pack_s(xq, 464, 512)
         quantize(xq, 2)
         multiply(wq, h_at, 2)
-        quantize(xq, 3)
-        multiply(wq, h_at, 3)
         for g in range(G):
             tanh(g, 0, 2)
         multiply(uq, g_at, 2)
+        quantize(xq, 3)
+        multiply(wq, h_at, 3)
         for g in range(G):
             gate(g, 0, 2)
             store(g, 0, 2)

@@ -18,7 +18,7 @@ P = 128
 PACK = 4
 ROWS = D // PACK
 NT = 128
-PAIR = 2
+PAIR = 4
 
 
 def tile_rows_gglu_tanh_kernel(tc, x, w, u, out):
@@ -51,8 +51,8 @@ def tile_rows_gglu_tanh_kernel(tc, x, w, u, out):
         banks = [[ps.tile([P, 512], F32, name="bank%d_%d" % (g, b)) for b in range(4)] for g in range(G)]
         act = [sb.tile([P, N], F32, name="act%d" % g) for g in range(G)]
         res = [sb.tile([P, N], F32, name="res%d" % g) for g in range(G)]
-        h_at = [(0, 0), (0, 128), (2, 0), (3, 0)]
-        g_at = [(1, 0), (1, 128), (0, 256), (2, 128)]
+        h_at = [(0, 0), (0, 128), (2, 0), (0, 256)]
+        g_at = [(1, 0), (1, 128), (3, 0), (2, 128)]
 
         def views(op, lo, hi):
             dst = op["packed"][:, lo:hi, :].rearrange("p (c i) j -> p c j i", i=PAIR)
@@ -132,29 +132,30 @@ def tile_rows_gglu_tanh_kernel(tc, x, w, u, out):
         multiply(wq, h_at, 1)
         pack_v(uq, 0, 80)
         pack_s(uq, 80, 128)
-        pack_v(xq, 256, 336)
-        pack_s(xq, 336, 384)
         quantize(uq, 0)
         multiply(uq, g_at, 0)
         multiply(uq, g_at, 1)
-        pack_v(xq, 384, 464)
-        pack_s(xq, 464, 512)
+        pack_v(xq, 256, 336)
+        pack_s(xq, 336, 384)
         quantize(xq, 2)
         multiply(wq, h_at, 2)
-        for g in range(G):
-            tanh(g, 0, 2)
         multiply(uq, g_at, 2)
+        tanh(0, 0, 2)
+        pack_v(xq, 384, 464)
+        pack_s(xq, 464, 512)
+        tanh(1, 0, 2)
+        gate(0, 0, 2)
+        store(0, 0, 2)
         quantize(xq, 3)
+        gate(1, 0, 2)
+        store(1, 0, 2)
         multiply(wq, h_at, 3)
         for g in range(G):
-            gate(g, 0, 2)
-            store(g, 0, 2)
-        for g in range(G):
             tanh(g, 2, 1)
+            gate(g, 2, 1)
+            store(g, 2, 1)
         multiply(uq, g_at, 3)
         for g in range(G):
             tanh(g, 3, 1)
-        for b in (2, 3):
-            for g in range(G):
-                gate(g, b, 1)
-                store(g, b, 1)
+            gate(g, 3, 1)
+            store(g, 3, 1)

@@ -41,16 +41,16 @@ def tile_rows_gglu_tanh_kernel(tc, x, w, u, out):
                 "scales": sb.tile([P, width], U8, name=name + "_scales", align_bytes=64),
             }
 
-        w_raw = sb.tile([P, PACK, M], F32, name="w_raw", align_bytes=64)
-        u_raw = sb.tile([P, PACK, M], F32, name="u_raw", align_bytes=64)
-        x_raw = sb.tile([P, 2, 2 * N], F32, name="x_raw", align_bytes=64)
+        w_raw = sb.tile([P, PACK, M], F32, name="w_raw", align_bytes=256)
+        u_raw = sb.tile([P, PACK, M], F32, name="u_raw", align_bytes=256)
+        x_raw = sb.tile([P, 2, 2 * N], F32, name="x_raw", align_bytes=256)
         x_four = x_raw[:].rearrange("p h (e n) -> p (h e) n", e=2)
         wq = operand("w", w_raw[:], M)
         uq = operand("u", u_raw[:], M)
         xq = operand("x", x_four, N)
         banks = [[ps.tile([P, 512], F32, name="bank%d_%d" % (g, b)) for b in range(4)] for g in range(G)]
         act = [sb.tile([P, N], F32, name="act%d" % g) for g in range(G)]
-        res = [sb.tile([P, N], F32, name="res%d" % g) for g in range(G)]
+        res = [sb.tile([P, N], F32, name="res%d" % g, align_bytes=256) for g in range(G)]
         h_at = [(0, 0), (0, 128), (2, 0), (0, 256)]
         g_at = [(1, 0), (1, 128), (3, 0), (2, 128)]
 

@@ -17,145 +17,154 @@ MULT = mybir.AluOpType.mult
 P = 128
 PACK = 4
 ROWS = D // PACK
-NT = 128
-PAIR = 4
+STRIP = 128
+BANK = 512
+BANKS_PER_GROUP = 4
+LINE = 4
+MX_ALIGN = 64
+DMA_ALIGN = 256
+
+VECTOR_SHARE = 88
+VECTOR_SHARE_FIRST = 192
+
+Z_AT = [(0, 0), (0, 1), (2, 0), (0, 2)]
+GATE_AT = [(1, 0), (1, 1), (3, 0), (2, 1)]
 
 
 def tile_rows_gglu_tanh_kernel(tc, x, w, u, out):
     nc = tc.nc
-    x_pairs = x.rearrange("g d n -> (g d) n").rearrange("(p h e) n -> p h (e n)", h=2, e=2)
-    x_rows = x.rearrange("g d n -> (g d) n").rearrange("(p j) n -> p j n", j=PACK)
-    w_rows = w.rearrange("g d m -> (g d) m").rearrange("(p j) m -> p j m", j=PACK)
-    u_rows = u.rearrange("g d m -> (g d) m").rearrange("(p j) m -> p j m", j=PACK)
+
+    def by_partition(t):
+        return t.rearrange("g d c -> (g d) c").rearrange("(p j) c -> p j c", j=PACK)
 
     with ExitStack() as ctx:
         sb = ctx.enter_context(tc.tile_pool(name="sb", bufs=1))
         ps = ctx.enter_context(tc.psum_pool(name="ps", bufs=1))
         ctx.enter_context(tc.manual_schedule())
 
+        w_raw = sb.tile([P, PACK, M], F32, name="w_raw", align_bytes=DMA_ALIGN)
+        u_raw = sb.tile([P, PACK, M], F32, name="u_raw", align_bytes=DMA_ALIGN)
+        x_raw = sb.tile([P, PACK, N], F32, name="x_raw", align_bytes=DMA_ALIGN)
+
         def operand(name, raw, width):
             return {
                 "raw": raw,
-                "packed": sb.tile([P, width, PACK], BF16, name=name + "_packed", align_bytes=64),
-                "codes": sb.tile([P, width], U32, name=name + "_codes", align_bytes=64),
-                "scales": sb.tile([P, width], U8, name=name + "_scales", align_bytes=64),
+                "packed": sb.tile([P, width, PACK], BF16, name=name + "_packed", align_bytes=MX_ALIGN),
+                "codes": sb.tile([P, width], U32, name=name + "_codes", align_bytes=MX_ALIGN),
+                "scales": sb.tile([P, width], U8, name=name + "_scales", align_bytes=MX_ALIGN),
             }
 
-        w_raw = sb.tile([P, PACK, M], F32, name="w_raw", align_bytes=256)
-        u_raw = sb.tile([P, PACK, M], F32, name="u_raw", align_bytes=256)
-        x_raw = sb.tile([P, 2, 2 * N], F32, name="x_raw", align_bytes=256)
-        x_four = x_raw[:].rearrange("p h (e n) -> p (h e) n", e=2)
-        wq = operand("w", w_raw[:], M)
-        uq = operand("u", u_raw[:], M)
-        xq = operand("x", x_four, N)
-        banks = [[ps.tile([P, 512], F32, name="bank%d_%d" % (g, b)) for b in range(4)] for g in range(G)]
-        act = [sb.tile([P, N], F32, name="act%d" % g) for g in range(G)]
-        res = [sb.tile([P, N], F32, name="res%d" % g, align_bytes=256) for g in range(G)]
-        h_at = [(0, 0), (0, 128), (2, 0), (0, 256)]
-        g_at = [(1, 0), (1, 128), (3, 0), (2, 128)]
+        wq = operand("w", w_raw, M)
+        uq = operand("u", u_raw, M)
+        xq = operand("x", x_raw, N)
+        banks = [
+            [ps.tile([P, BANK], F32, name="bank%d_%d" % (grp, b)) for b in range(BANKS_PER_GROUP)] for grp in range(G)
+        ]
+        tanh_z = [sb.tile([P, N], F32, name="tanh_z%d" % grp) for grp in range(G)]
+        result = [sb.tile([P, N], F32, name="result%d" % grp, align_bytes=DMA_ALIGN) for grp in range(G)]
 
-        def views(op, lo, hi):
-            dst = op["packed"][:, lo:hi, :].rearrange("p (c i) j -> p c j i", i=PAIR)
-            src = op["raw"][:, :, lo:hi].rearrange("p j (c i) -> p c j i", i=PAIR)
+        def strips(first, count=1):
+            return slice(STRIP * first, STRIP * (first + count))
+
+        def sums(place, grp, first, count=1):
+            bank, at = place[first]
+            return banks[grp][bank][:, strips(at, count)]
+
+        def interleaving(op, lo, hi):
+            dst = op["packed"][:, lo:hi, :].rearrange("p (c i) j -> p c j i", i=LINE)
+            src = op["raw"][:, :, lo:hi].rearrange("p j (c i) -> p c j i", i=LINE)
             return dst, src
 
-        def pack_v(op, lo, hi):
-            dst, src = views(op, lo, hi)
+        def pack(op, strip):
+            lo = STRIP * strip
+            dst, src = interleaving(op, lo, lo + VECTOR_SHARE)
             nc.vector.tensor_copy(out=dst, in_=src)
-
-        def pack_s(op, lo, hi):
-            dst, src = views(op, lo, hi)
+            dst, src = interleaving(op, lo + VECTOR_SHARE, lo + STRIP)
             nc.scalar.copy(out=dst, in_=src)
 
-        def pack_a(op, lo, hi):
-            dst, src = views(op, lo, hi)
-            nc.scalar.activation(out=dst, in_=src, func=COPY)
-
-        def quantize(op, b, count=1):
-            lo, hi = NT * b, NT * (b + count)
+        def quantize(op, first, count=1):
+            cols = strips(first, count)
             nc.vector.quantize_mx(
-                out=op["codes"][:, lo:hi].bitcast(FP8X4),
-                scales=op["scales"][:, lo:hi],
-                in_=op["packed"][:, lo:hi, :].rearrange("p c j -> p (c j)"),
+                out=op["codes"][:, cols].bitcast(FP8X4),
+                scales=op["scales"][:, cols],
+                in_=op["packed"][:, cols, :].rearrange("p c j -> p (c j)"),
             )
 
-        def multiply(weights, place, b, groups=(0, 1)):
-            cols = slice(NT * b, NT * (b + 1))
-            bank, first = place[b]
-            for g in groups:
-                rows = slice(ROWS * g, ROWS * (g + 1))
+        def multiply(weights, place, strip):
+            for grp in range(G):
+                rows = slice(ROWS * grp, ROWS * (grp + 1))
                 nc.tensor.matmul_mx(
-                    out=banks[g][bank][:, first : first + NT],
+                    out=sums(place, grp, strip),
                     lhsT=weights["codes"][rows, :].bitcast(FP8X4),
                     lhsT_scale=weights["scales"][rows, :],
-                    rhs=xq["codes"][rows, cols].bitcast(FP8X4),
-                    rhs_scale=xq["scales"][rows, cols],
+                    rhs=xq["codes"][rows, strips(strip)].bitcast(FP8X4),
+                    rhs_scale=xq["scales"][rows, strips(strip)],
                     start=True,
                     stop=True,
                 )
 
-        def tanh(g, b, count):
-            bank, first = h_at[b]
-            nc.scalar.activation(
-                out=act[g][:, NT * b : NT * (b + count)], in_=banks[g][bank][:, first : first + NT * count], func=TANH
-            )
+        def activate(grp, first, count=1):
+            nc.scalar.activation(out=tanh_z[grp][:, strips(first, count)], in_=sums(Z_AT, grp, first, count), func=TANH)
 
-        def gate(g, b, count):
-            bank, first = g_at[b]
-            cols = slice(NT * b, NT * (b + count))
+        def apply_gate(grp, first, count=1):
+            cols = strips(first, count)
             nc.vector.tensor_tensor(
-                out=res[g][:, cols], in0=banks[g][bank][:, first : first + NT * count], in1=act[g][:, cols], op=MULT
+                out=result[grp][:, cols], in0=sums(GATE_AT, grp, first, count), in1=tanh_z[grp][:, cols], op=MULT
             )
 
-        def store(g, b, count, eng=None):
-            cols = slice(NT * b, NT * (b + count))
-            (eng or nc.sync).dma_start(out=out[g, :, cols], in_=res[g][:, cols])
+        def store(grp, first, count=1, queue=nc.sync):
+            cols = strips(first, count)
+            queue.dma_start(out=out[grp, :, cols], in_=result[grp][:, cols])
 
-        def load_x(lo, hi):
-            nc.sync.dma_start(out=x_raw[:, :, lo:hi], in_=x_pairs[:, :, lo:hi])
+        def load_x(first, count=1):
+            cols = strips(first, count)
+            nc.sync.dma_start(out=x_raw[:, :, cols], in_=by_partition(x)[:, :, cols])
 
-        def load_cols(lo, hi):
-            nc.sync.dma_start(out=x_four[:, :, lo:hi], in_=x_rows[:, :, lo:hi])
+        load_x(0, 2)
+        nc.sync.dma_start(out=w_raw[:], in_=by_partition(w))
+        nc.sync.dma_start(out=u_raw[:], in_=by_partition(u))
+        load_x(2)
+        load_x(3)
 
-        load_cols(0, 256)
-        nc.sync.dma_start(out=w_raw[:], in_=w_rows)
-        nc.sync.dma_start(out=u_raw[:], in_=u_rows)
-        load_cols(256, 384)
-        load_cols(384, 512)
-        pack_v(xq, 0, 192)
-        pack_a(xq, 192, 256)
-        pack_v(wq, 0, 80)
-        pack_s(wq, 80, 128)
+        dst, src = interleaving(xq, 0, VECTOR_SHARE_FIRST)
+        nc.vector.tensor_copy(out=dst, in_=src)
+        dst, src = interleaving(xq, VECTOR_SHARE_FIRST, 2 * STRIP)
+        nc.scalar.activation(out=dst, in_=src, func=COPY)
+
+        pack(wq, 0)
         quantize(xq, 0, 2)
         quantize(wq, 0)
-        multiply(wq, h_at, 0)
-        multiply(wq, h_at, 1)
-        pack_v(uq, 0, 80)
-        pack_s(uq, 80, 128)
+        multiply(wq, Z_AT, 0)
+        multiply(wq, Z_AT, 1)
+
+        pack(uq, 0)
         quantize(uq, 0)
-        multiply(uq, g_at, 0)
-        multiply(uq, g_at, 1)
-        pack_v(xq, 256, 336)
-        pack_s(xq, 336, 384)
+        multiply(uq, GATE_AT, 0)
+        multiply(uq, GATE_AT, 1)
+
+        pack(xq, 2)
         quantize(xq, 2)
-        multiply(wq, h_at, 2)
-        multiply(uq, g_at, 2)
-        tanh(0, 0, 2)
-        pack_v(xq, 384, 464)
-        pack_s(xq, 464, 512)
-        tanh(1, 0, 2)
-        gate(0, 0, 2)
-        store(0, 0, 2)
+        multiply(wq, Z_AT, 2)
+        multiply(uq, GATE_AT, 2)
+
+        activate(0, 0, 2)
+        pack(xq, 3)
+        activate(1, 0, 2)
+        apply_gate(0, 0)
         quantize(xq, 3)
-        gate(1, 0, 2)
+        apply_gate(0, 1)
+        store(0, 0, 2)
+        apply_gate(1, 0, 2)
         store(1, 0, 2)
-        multiply(wq, h_at, 3)
-        for g in range(G):
-            tanh(g, 2, 1)
-            gate(g, 2, 1)
-            store(g, 2, 1)
-        multiply(uq, g_at, 3)
-        for g in range(G):
-            tanh(g, 3, 1)
-            gate(g, 3, 1)
-            store(g, 3, 1)
+
+        multiply(wq, Z_AT, 3)
+        for grp in range(G):
+            activate(grp, 2)
+            apply_gate(grp, 2)
+            store(grp, 2)
+        multiply(uq, GATE_AT, 3)
+        for grp in range(G):
+            activate(grp, 3)
+            apply_gate(grp, 3)
+        store(0, 3)
+        store(1, 3, queue=nc.scalar)

@@ -24,12 +24,6 @@ LINE = 4
 MX_ALIGN = 64
 DMA_ALIGN = 256
 
-VECTOR_SHARE = 88
-VECTOR_SHARE_FIRST = 192
-
-Z_AT = [(0, 0), (0, 1), (2, 0), (0, 2)]
-GATE_AT = [(1, 0), (1, 1), (3, 0), (2, 1)]
-
 
 def tile_rows_gglu_tanh_kernel(tc, x, w, u, out):
     nc = tc.nc
@@ -54,117 +48,117 @@ def tile_rows_gglu_tanh_kernel(tc, x, w, u, out):
                 "scales": sb.tile([P, width], U8, name=name + "_scales", align_bytes=MX_ALIGN),
             }
 
-        wq = operand("w", w_raw, M)
-        uq = operand("u", u_raw, M)
-        xq = operand("x", x_raw, N)
+        ops = {"w": operand("w", w_raw, M), "u": operand("u", u_raw, M), "x": operand("x", x_raw, N)}
+        dram = {"w": w, "u": u, "x": x}
         banks = [
             [ps.tile([P, BANK], F32, name="bank%d_%d" % (grp, b)) for b in range(BANKS_PER_GROUP)] for grp in range(G)
         ]
         tanh_z = [sb.tile([P, N], F32, name="tanh_z%d" % grp) for grp in range(G)]
-        result = [sb.tile([P, N], F32, name="result%d" % grp, align_bytes=DMA_ALIGN) for grp in range(G)]
+        result_all = sb.tile([P, G, N], F32, name="result", align_bytes=DMA_ALIGN)
+        place = {}
+        queues = {"sync": nc.sync, "scalar": nc.scalar}
+        scalar_used = []
 
-        def strips(first, count=1):
-            return slice(STRIP * first, STRIP * (first + count))
+        def places(z_at, gate_at):
+            place["w"] = z_at
+            place["u"] = gate_at
 
-        def sums(place, grp, first, count=1):
-            bank, at = place[first]
-            return banks[grp][bank][:, strips(at, count)]
+        def sums(name, grp, lo, hi):
+            bank, at = place[name][lo // STRIP]
+            start = STRIP * at + lo % STRIP
+            return banks[grp][bank][:, start : start + hi - lo]
 
-        def interleaving(op, lo, hi):
+        def copy(engine, name, lo, hi):
+            op = ops[name]
             dst = op["packed"][:, lo:hi, :].rearrange("p (c i) j -> p c j i", i=LINE)
             src = op["raw"][:, :, lo:hi].rearrange("p j (c i) -> p c j i", i=LINE)
-            return dst, src
+            if engine == "vector":
+                nc.vector.tensor_copy(out=dst, in_=src)
+            elif scalar_used:
+                nc.scalar.copy(out=dst, in_=src)
+            else:
+                scalar_used.append(1)
+                nc.scalar.activation(out=dst, in_=src, func=COPY)
 
-        def pack(op, strip):
-            lo = STRIP * strip
-            dst, src = interleaving(op, lo, lo + VECTOR_SHARE)
-            nc.vector.tensor_copy(out=dst, in_=src)
-            dst, src = interleaving(op, lo + VECTOR_SHARE, lo + STRIP)
-            nc.scalar.copy(out=dst, in_=src)
-
-        def quantize(op, first, count=1):
-            cols = strips(first, count)
+        def quantize(name, lo, hi):
+            op = ops[name]
             nc.vector.quantize_mx(
-                out=op["codes"][:, cols].bitcast(FP8X4),
-                scales=op["scales"][:, cols],
-                in_=op["packed"][:, cols, :].rearrange("p c j -> p (c j)"),
+                out=op["codes"][:, lo:hi].bitcast(FP8X4),
+                scales=op["scales"][:, lo:hi],
+                in_=op["packed"][:, lo:hi, :].rearrange("p c j -> p (c j)"),
             )
 
-        def multiply(weights, place, strip):
+        def mm(name, strip, grp):
+            rows = slice(ROWS * grp, ROWS * (grp + 1))
+            cols = slice(STRIP * strip, STRIP * (strip + 1))
+            nc.tensor.matmul_mx(
+                out=sums(name, grp, cols.start, cols.stop),
+                lhsT=ops[name]["codes"][rows, :].bitcast(FP8X4),
+                lhsT_scale=ops[name]["scales"][rows, :],
+                rhs=ops["x"]["codes"][rows, cols].bitcast(FP8X4),
+                rhs_scale=ops["x"]["scales"][rows, cols],
+                start=True,
+                stop=True,
+            )
+
+        def multiply(name, strip):
             for grp in range(G):
-                rows = slice(ROWS * grp, ROWS * (grp + 1))
-                nc.tensor.matmul_mx(
-                    out=sums(place, grp, strip),
-                    lhsT=weights["codes"][rows, :].bitcast(FP8X4),
-                    lhsT_scale=weights["scales"][rows, :],
-                    rhs=xq["codes"][rows, strips(strip)].bitcast(FP8X4),
-                    rhs_scale=xq["scales"][rows, strips(strip)],
-                    start=True,
-                    stop=True,
-                )
+                mm(name, strip, grp)
 
-        def activate(grp, first, count=1):
-            nc.scalar.activation(out=tanh_z[grp][:, strips(first, count)], in_=sums(Z_AT, grp, first, count), func=TANH)
+        def activate(grp, lo, hi):
+            nc.scalar.activation(out=tanh_z[grp][:, lo:hi], in_=sums("w", grp, lo, hi), func=TANH)
 
-        def apply_gate(grp, first, count=1):
-            cols = strips(first, count)
+        def gate(grp, lo, hi):
             nc.vector.tensor_tensor(
-                out=result[grp][:, cols], in0=sums(GATE_AT, grp, first, count), in1=tanh_z[grp][:, cols], op=MULT
+                out=result_all[:, grp, lo:hi], in0=sums("u", grp, lo, hi), in1=tanh_z[grp][:, lo:hi], op=MULT
             )
 
-        def store(grp, first, count=1, queue=nc.sync):
-            cols = strips(first, count)
-            queue.dma_start(out=out[grp, :, cols], in_=result[grp][:, cols])
+        def store(grp, lo, hi, queue="sync"):
+            queues[queue].dma_start(out=out[grp, :, lo:hi], in_=result_all[:, grp, lo:hi])
 
-        def load_x(first, count=1):
-            cols = strips(first, count)
-            nc.sync.dma_start(out=x_raw[:, :, cols], in_=by_partition(x)[:, :, cols])
+        def store2(lo, hi, queue="sync"):
+            queues[queue].dma_start(out=out[:, :, lo:hi].rearrange("g m n -> m g n"), in_=result_all[:, :, lo:hi])
 
-        load_x(0, 2)
-        nc.sync.dma_start(out=w_raw[:], in_=by_partition(w))
-        nc.sync.dma_start(out=u_raw[:], in_=by_partition(u))
-        load_x(2)
-        load_x(3)
+        def load_w(name, queue="sync"):
+            queues[queue].dma_start(out=ops[name]["raw"][:], in_=by_partition(dram[name]))
 
-        dst, src = interleaving(xq, 0, VECTOR_SHARE_FIRST)
-        nc.vector.tensor_copy(out=dst, in_=src)
-        dst, src = interleaving(xq, VECTOR_SHARE_FIRST, 2 * STRIP)
-        nc.scalar.activation(out=dst, in_=src, func=COPY)
+        def load_x(lo, hi, queue="sync"):
+            queues[queue].dma_start(out=x_raw[:, :, lo:hi], in_=by_partition(x)[:, :, lo:hi])
 
-        pack(wq, 0)
-        quantize(xq, 0, 2)
-        quantize(wq, 0)
-        multiply(wq, Z_AT, 0)
-        multiply(wq, Z_AT, 1)
+        def pairs(t):
+            return t.rearrange("p (a b) c -> p a (b c)", b=2)
 
-        pack(uq, 0)
-        quantize(uq, 0)
-        multiply(uq, GATE_AT, 0)
-        multiply(uq, GATE_AT, 1)
+        def load_x_long(hi, queue="sync"):
+            queues[queue].dma_start(out=pairs(x_raw[:])[:, :, : N + hi], in_=pairs(by_partition(x))[:, :, : N + hi])
 
-        pack(xq, 2)
-        quantize(xq, 2)
-        multiply(wq, Z_AT, 2)
-        multiply(uq, GATE_AT, 2)
+        def load_x_run(hi, queue="sync"):
+            queues[queue].dma_start(out=pairs(x_raw[:])[:, 0, : N + hi], in_=pairs(by_partition(x))[:, 0, : N + hi])
 
-        activate(0, 0, 2)
-        pack(xq, 3)
-        activate(1, 0, 2)
-        apply_gate(0, 0)
-        quantize(xq, 3)
-        apply_gate(0, 1)
-        store(0, 0, 2)
-        apply_gate(1, 0, 2)
-        store(1, 0, 2)
+        def load_x_rows(j0, j1, lo, hi, queue="sync"):
+            queues[queue].dma_start(out=x_raw[:, j0:j1, lo:hi], in_=by_partition(x)[:, j0:j1, lo:hi])
 
-        multiply(wq, Z_AT, 3)
-        for grp in range(G):
-            activate(grp, 2)
-            apply_gate(grp, 2)
-            store(grp, 2)
-        multiply(uq, GATE_AT, 3)
-        for grp in range(G):
-            activate(grp, 3)
-            apply_gate(grp, 3)
-        store(0, 3)
-        store(1, 3, queue=nc.scalar)
+        def load_x_odd(lo, hi, queue="sync"):
+            queues[queue].dma_start(
+                out=pairs(x_raw[:])[:, :, N + lo : N + hi], in_=pairs(by_partition(x))[:, :, N + lo : N + hi]
+            )
+
+        places([(0, 0), (0, 1), (2, 0), (0, 2)], [(1, 0), (1, 1), (3, 0), (2, 1)])
+
+        def pack(n, lo, v=88, w=128):
+            if v>0: copy('vector',n,lo,lo+v)
+            if v<w: copy('scalar',n,lo+v,lo+w)
+        load_x(0,256); load_w('w'); load_w('u'); load_x(256,384); load_x(384,512)
+
+        pack('x',0,192,256)
+        pack('w',0); quantize('x',0,256); quantize('w',0,128); multiply('w',0); multiply('w',1)
+        copy('vector','u',0,64); copy('vector','u',64,96); copy('scalar','u',96,128); quantize('u',0,64); quantize('u',64,128); multiply('u',0); multiply('u',1)
+        copy('vector','x',256,320); copy('vector','x',320,352); copy('scalar','x',352,384); quantize('x',256,320); quantize('x',320,384); multiply('w',2); multiply('u',2)
+        activate(0,0,256); copy('vector','x',384,448); copy('vector','x',448,480); copy('scalar','x',480,512); activate(1,0,256); quantize('x',384,448); quantize('x',448,512); gate(0,0,256); store(0,0,256); gate(1,0,256); store(1,0,256)
+
+        multiply('w',3)
+        for g in range(2):
+            activate(g,256,384); gate(g,256,384); store(g,256,384)
+        multiply('u',3)
+        for g in range(2):
+            activate(g,384,512); gate(g,384,512)
+        store(0,384,512); store(1,384,512,'scalar')

@@ -151,8 +151,8 @@ def tile_rows_gglu_tanh_kernel(tc, x, w, u, out):
 
         pack('x',0,192,256)
         pack('w',0); quantize('x',0,256); quantize('w',0,128); multiply('w',0); multiply('w',1)
-        copy('vector','u',0,64); copy('vector','u',64,96); copy('scalar','u',96,128); quantize('u',0,64); quantize('u',64,128); multiply('u',0); multiply('u',1)
-        copy('vector','x',256,320); copy('vector','x',320,352); copy('scalar','x',352,384); quantize('x',256,320); quantize('x',320,384); multiply('w',2); multiply('u',2)
+        copy('vector','u',0,64); copy('scalar','u',64,128); quantize('u',0,64); quantize('u',64,128); multiply('u',0); multiply('u',1)
+        copy('vector','x',256,320); copy('scalar','x',320,384); quantize('x',256,320); quantize('x',320,384); multiply('w',2); multiply('u',2)
         activate(0,0,256); copy('vector','x',384,448); copy('vector','x',448,480); copy('scalar','x',480,512); activate(1,0,256); quantize('x',384,448); quantize('x',448,512); gate(0,0,256); store(0,0,256); gate(1,0,256); store(1,0,256)
 
         multiply('w',3)

@@ -59,12 +59,12 @@ def tile_rows_gglu_tanh_kernel(tc, x, w, u, out):
         queues = {"sync": nc.sync, "scalar": nc.scalar}
         scalar_used = []
 
-        def places(z_at, gate_at):
-            place["w"] = z_at
-            place["u"] = gate_at
+        def places(z_at, gate_at, z_at1=None, gate_at1=None):
+            place["w"] = [z_at, z_at1 or z_at]
+            place["u"] = [gate_at, gate_at1 or gate_at]
 
         def sums(name, grp, lo, hi):
-            bank, at = place[name][lo // STRIP]
+            bank, at = place[name][grp][lo // STRIP]
             start = STRIP * at + lo % STRIP
             return banks[grp][bank][:, start : start + hi - lo]
 
@@ -142,7 +142,7 @@ def tile_rows_gglu_tanh_kernel(tc, x, w, u, out):
                 out=pairs(x_raw[:])[:, :, N + lo : N + hi], in_=pairs(by_partition(x))[:, :, N + lo : N + hi]
             )
 
-        places([(0, 0), (0, 1), (2, 0), (0, 2)], [(1, 0), (1, 1), (3, 0), (2, 1)])
+        places([(0, 0), (2, 0), (3, 0), (1, 1)], [(1, 0), (2, 1), (0, 1), (3, 1)], [(0, 0), (0, 1), (2, 0), (0, 2)], [(1, 0), (1, 1), (3, 0), (2, 1)])
 
         def pack(n, lo, v=88, w=128):
             if v>0: copy('vector',n,lo,lo+v)
@@ -152,12 +152,10 @@ def tile_rows_gglu_tanh_kernel(tc, x, w, u, out):
         pack('x',0,192,256)
         pack('w',0); quantize('x',0,256); quantize('w',0,128); multiply('w',0); multiply('w',1)
         copy('vector','u',0,64); copy('scalar','u',64,128); quantize('u',0,64); quantize('u',64,128); multiply('u',0); multiply('u',1)
-        copy('vector','x',256,320); copy('scalar','x',320,384); quantize('x',256,320); quantize('x',320,384); multiply('w',2); multiply('u',2)
-        activate(0,0,256); copy('vector','x',384,448); copy('vector','x',448,480); copy('scalar','x',480,512); activate(1,0,256); quantize('x',384,448); quantize('x',448,512); gate(0,0,256); store(0,0,256); gate(1,0,256); store(1,0,256)
-
+        copy('vector','x',256,320); copy('scalar','x',320,384); quantize('x',256,320); quantize('x',320,384); activate(0,0,128); multiply('w',2); multiply('u',2)
+        copy('vector','x',384,448); copy('scalar','x',448,512); activate(1,0,256); activate(0,128,256); gate(0,0,128); store(0,0,128); quantize('x',384,448); quantize('x',448,512); gate(1,0,256); store(1,0,256); gate(0,128,256)
         multiply('w',3)
-        for g in range(2):
-            activate(g,256,384); gate(g,256,384); store(g,256,384)
+        activate(0,256,384); gate(0,256,384); store(0,128,384); activate(1,256,384); gate(1,256,384); store(1,256,384)
         multiply('u',3)
         for g in range(2):
             activate(g,384,512); gate(g,384,512)

@@ -149,8 +149,8 @@ def tile_rows_gglu_tanh_kernel(tc, x, w, u, out):
             if v<w: copy('scalar',n,lo+v,lo+w)
         load_x(0,256); load_w('w'); load_w('u'); load_x(256,384); load_x(384,512)
 
-        pack('x',0,192,256)
-        pack('w',0); quantize('x',0,256); quantize('w',0,128); multiply('w',0); multiply('w',1)
+        copy('vector','x',0,64); copy('vector','x',64,160); copy('scalar','x',160,256); quantize('x',0,64)
+        copy('vector','w',0,64); copy('scalar','w',64,128); quantize('x',64,128); quantize('x',128,256); quantize('w',0,64); quantize('w',64,128); multiply('w',0); multiply('w',1)
         copy('vector','u',0,64); copy('scalar','u',64,128); quantize('u',0,64); quantize('u',64,128); multiply('u',0); multiply('u',1)
         copy('vector','x',256,320); copy('scalar','x',320,384); quantize('x',256,320); quantize('x',320,384); activate(0,0,128); multiply('w',2); multiply('u',2)
         copy('vector','x',384,448); copy('scalar','x',448,512); activate(1,0,256); activate(0,128,256); gate(0,0,128); store(0,0,128); quantize('x',384,448); quantize('x',448,512); gate(1,0,256); store(1,0,256); gate(0,128,256)

@@ -18,11 +18,19 @@ P = 128
 PACK = 4
 ROWS = D // PACK
 STRIP = 128
+HALF = STRIP // 2
 BANK = 512
 BANKS_PER_GROUP = 4
 LINE = 4
 MX_ALIGN = 64
 DMA_ALIGN = 256
+
+VECTOR_SHARE_FIRST = 160
+
+VECTOR_SHARE_TOGETHER = 72
+
+Z_AT = [[(0, 0), (2, 0), (3, 0), (1, 1)], [(0, 0), (0, 1), (2, 0), (0, 2)]]
+GATE_AT = [[(1, 0), (2, 1), (0, 1), (3, 1)], [(1, 0), (1, 1), (3, 0), (2, 1)]]
 
 
 def tile_rows_gglu_tanh_kernel(tc, x, w, u, out):
@@ -48,115 +56,135 @@ def tile_rows_gglu_tanh_kernel(tc, x, w, u, out):
                 "scales": sb.tile([P, width], U8, name=name + "_scales", align_bytes=MX_ALIGN),
             }
 
-        ops = {"w": operand("w", w_raw, M), "u": operand("u", u_raw, M), "x": operand("x", x_raw, N)}
-        dram = {"w": w, "u": u, "x": x}
+        wq = operand("w", w_raw, M)
+        uq = operand("u", u_raw, M)
+        xq = operand("x", x_raw, N)
         banks = [
             [ps.tile([P, BANK], F32, name="bank%d_%d" % (grp, b)) for b in range(BANKS_PER_GROUP)] for grp in range(G)
         ]
         tanh_z = [sb.tile([P, N], F32, name="tanh_z%d" % grp) for grp in range(G)]
-        result_all = sb.tile([P, G, N], F32, name="result", align_bytes=DMA_ALIGN)
-        place = {}
-        queues = {"sync": nc.sync, "scalar": nc.scalar}
-        scalar_used = []
+        result = sb.tile([P, G, N], F32, name="result", align_bytes=DMA_ALIGN)
 
-        def places(z_at, gate_at, z_at1=None, gate_at1=None):
-            place["w"] = [z_at, z_at1 or z_at]
-            place["u"] = [gate_at, gate_at1 or gate_at]
+        def strips(first, count=1):
+            return slice(STRIP * first, STRIP * (first + count))
 
-        def sums(name, grp, lo, hi):
-            bank, at = place[name][grp][lo // STRIP]
-            start = STRIP * at + lo % STRIP
-            return banks[grp][bank][:, start : start + hi - lo]
+        def first_half(strip):
+            return slice(STRIP * strip, STRIP * strip + HALF)
 
-        def copy(engine, name, lo, hi):
-            op = ops[name]
-            dst = op["packed"][:, lo:hi, :].rearrange("p (c i) j -> p c j i", i=LINE)
-            src = op["raw"][:, :, lo:hi].rearrange("p j (c i) -> p c j i", i=LINE)
-            if engine == "vector":
-                nc.vector.tensor_copy(out=dst, in_=src)
-            elif scalar_used:
-                nc.scalar.copy(out=dst, in_=src)
-            else:
-                scalar_used.append(1)
-                nc.scalar.activation(out=dst, in_=src, func=COPY)
+        def second_half(strip):
+            return slice(STRIP * strip + HALF, STRIP * (strip + 1))
 
-        def quantize(name, lo, hi):
-            op = ops[name]
+        def sums(place, grp, first, count=1):
+            bank, at = place[grp][first]
+            return banks[grp][bank][:, strips(at, count)]
+
+        def interleaving(op, cols):
+            dst = op["packed"][:, cols, :].rearrange("p (c i) j -> p c j i", i=LINE)
+            src = op["raw"][:, :, cols].rearrange("p j (c i) -> p c j i", i=LINE)
+            return dst, src
+
+        def pack_on_vector(op, cols):
+            dst, src = interleaving(op, cols)
+            nc.vector.tensor_copy(out=dst, in_=src)
+
+        def pack(op, strip, vector_share):
+            cut = STRIP * strip + vector_share
+            pack_on_vector(op, slice(STRIP * strip, cut))
+            dst, src = interleaving(op, slice(cut, STRIP * (strip + 1)))
+            nc.scalar.copy(out=dst, in_=src)
+
+        def quantize(op, cols):
             nc.vector.quantize_mx(
-                out=op["codes"][:, lo:hi].bitcast(FP8X4),
-                scales=op["scales"][:, lo:hi],
-                in_=op["packed"][:, lo:hi, :].rearrange("p c j -> p (c j)"),
+                out=op["codes"][:, cols].bitcast(FP8X4),
+                scales=op["scales"][:, cols],
+                in_=op["packed"][:, cols, :].rearrange("p c j -> p (c j)"),
             )
 
-        def mm(name, strip, grp):
-            rows = slice(ROWS * grp, ROWS * (grp + 1))
-            cols = slice(STRIP * strip, STRIP * (strip + 1))
-            nc.tensor.matmul_mx(
-                out=sums(name, grp, cols.start, cols.stop),
-                lhsT=ops[name]["codes"][rows, :].bitcast(FP8X4),
-                lhsT_scale=ops[name]["scales"][rows, :],
-                rhs=ops["x"]["codes"][rows, cols].bitcast(FP8X4),
-                rhs_scale=ops["x"]["scales"][rows, cols],
-                start=True,
-                stop=True,
-            )
+        def quantize_halves(op, strip):
+            quantize(op, first_half(strip))
+            quantize(op, second_half(strip))
 
-        def multiply(name, strip):
+        def multiply(weights, place, strip):
             for grp in range(G):
-                mm(name, strip, grp)
+                rows = slice(ROWS * grp, ROWS * (grp + 1))
+                nc.tensor.matmul_mx(
+                    out=sums(place, grp, strip),
+                    lhsT=weights["codes"][rows, :].bitcast(FP8X4),
+                    lhsT_scale=weights["scales"][rows, :],
+                    rhs=xq["codes"][rows, strips(strip)].bitcast(FP8X4),
+                    rhs_scale=xq["scales"][rows, strips(strip)],
+                    start=True,
+                    stop=True,
+                )
 
-        def activate(grp, lo, hi):
-            nc.scalar.activation(out=tanh_z[grp][:, lo:hi], in_=sums("w", grp, lo, hi), func=TANH)
+        def activate(grp, first, count=1):
+            nc.scalar.activation(out=tanh_z[grp][:, strips(first, count)], in_=sums(Z_AT, grp, first, count), func=TANH)
 
-        def gate(grp, lo, hi):
+        def apply_gate(grp, first, count=1):
+            cols = strips(first, count)
             nc.vector.tensor_tensor(
-                out=result_all[:, grp, lo:hi], in0=sums("u", grp, lo, hi), in1=tanh_z[grp][:, lo:hi], op=MULT
+                out=result[:, grp, cols], in0=sums(GATE_AT, grp, first, count), in1=tanh_z[grp][:, cols], op=MULT
             )
 
-        def store(grp, lo, hi, queue="sync"):
-            queues[queue].dma_start(out=out[grp, :, lo:hi], in_=result_all[:, grp, lo:hi])
+        def store(grp, first, count=1, queue=nc.sync):
+            cols = strips(first, count)
+            queue.dma_start(out=out[grp, :, cols], in_=result[:, grp, cols])
 
-        def store2(lo, hi, queue="sync"):
-            queues[queue].dma_start(out=out[:, :, lo:hi].rearrange("g m n -> m g n"), in_=result_all[:, :, lo:hi])
+        def load_x(first, count=1):
+            cols = strips(first, count)
+            nc.sync.dma_start(out=x_raw[:, :, cols], in_=by_partition(x)[:, :, cols])
 
-        def load_w(name, queue="sync"):
-            queues[queue].dma_start(out=ops[name]["raw"][:], in_=by_partition(dram[name]))
+        load_x(0, 2)
+        nc.sync.dma_start(out=w_raw[:], in_=by_partition(w))
+        nc.sync.dma_start(out=u_raw[:], in_=by_partition(u))
+        load_x(2)
+        load_x(3)
 
-        def load_x(lo, hi, queue="sync"):
-            queues[queue].dma_start(out=x_raw[:, :, lo:hi], in_=by_partition(x)[:, :, lo:hi])
+        pack_on_vector(xq, first_half(0))
+        pack_on_vector(xq, slice(HALF, VECTOR_SHARE_FIRST))
+        dst, src = interleaving(xq, slice(VECTOR_SHARE_FIRST, 2 * STRIP))
+        nc.scalar.activation(out=dst, in_=src, func=COPY)
+        quantize(xq, first_half(0))
 
-        def pairs(t):
-            return t.rearrange("p (a b) c -> p a (b c)", b=2)
+        pack(wq, 0, VECTOR_SHARE_TOGETHER)
+        quantize(xq, second_half(0))
+        quantize(xq, strips(1))
+        quantize_halves(wq, 0)
+        multiply(wq, Z_AT, 0)
+        multiply(wq, Z_AT, 1)
 
-        def load_x_long(hi, queue="sync"):
-            queues[queue].dma_start(out=pairs(x_raw[:])[:, :, : N + hi], in_=pairs(by_partition(x))[:, :, : N + hi])
+        pack(uq, 0, HALF)
+        quantize_halves(uq, 0)
+        multiply(uq, GATE_AT, 0)
+        multiply(uq, GATE_AT, 1)
 
-        def load_x_run(hi, queue="sync"):
-            queues[queue].dma_start(out=pairs(x_raw[:])[:, 0, : N + hi], in_=pairs(by_partition(x))[:, 0, : N + hi])
+        pack(xq, 2, HALF)
+        quantize_halves(xq, 2)
+        activate(0, 0)
+        multiply(wq, Z_AT, 2)
+        multiply(uq, GATE_AT, 2)
 
-        def load_x_rows(j0, j1, lo, hi, queue="sync"):
-            queues[queue].dma_start(out=x_raw[:, j0:j1, lo:hi], in_=by_partition(x)[:, j0:j1, lo:hi])
+        pack(xq, 3, VECTOR_SHARE_TOGETHER)
+        activate(1, 0, 2)
+        activate(0, 1)
+        apply_gate(0, 0)
+        store(0, 0)
+        quantize_halves(xq, 3)
+        apply_gate(1, 0, 2)
+        store(1, 0, 2)
+        apply_gate(0, 1)
 
-        def load_x_odd(lo, hi, queue="sync"):
-            queues[queue].dma_start(
-                out=pairs(x_raw[:])[:, :, N + lo : N + hi], in_=pairs(by_partition(x))[:, :, N + lo : N + hi]
-            )
+        multiply(wq, Z_AT, 3)
+        activate(0, 2)
+        apply_gate(0, 2)
+        store(0, 1, 2)
+        activate(1, 2)
+        apply_gate(1, 2)
+        store(1, 2)
 
-        places([(0, 0), (2, 0), (3, 0), (1, 1)], [(1, 0), (2, 1), (0, 1), (3, 1)], [(0, 0), (0, 1), (2, 0), (0, 2)], [(1, 0), (1, 1), (3, 0), (2, 1)])
-
-        def pack(n, lo, v=88, w=128):
-            if v>0: copy('vector',n,lo,lo+v)
-            if v<w: copy('scalar',n,lo+v,lo+w)
-        load_x(0,256); load_w('w'); load_w('u'); load_x(256,384); load_x(384,512)
-
-        copy('vector','x',0,64); copy('vector','x',64,160); copy('scalar','x',160,256); quantize('x',0,64)
-        copy('vector','w',0,64); copy('scalar','w',64,128); quantize('x',64,128); quantize('x',128,256); quantize('w',0,64); quantize('w',64,128); multiply('w',0); multiply('w',1)
-        copy('vector','u',0,64); copy('scalar','u',64,128); quantize('u',0,64); quantize('u',64,128); multiply('u',0); multiply('u',1)
-        copy('vector','x',256,320); copy('scalar','x',320,384); quantize('x',256,320); quantize('x',320,384); activate(0,0,128); multiply('w',2); multiply('u',2)
-        copy('vector','x',384,448); copy('scalar','x',448,512); activate(1,0,256); activate(0,128,256); gate(0,0,128); store(0,0,128); quantize('x',384,448); quantize('x',448,512); gate(1,0,256); store(1,0,256); gate(0,128,256)
-        multiply('w',3)
-        activate(0,256,384); gate(0,256,384); store(0,128,384); activate(1,256,384); gate(1,256,384); store(1,256,384)
-        multiply('u',3)
-        for g in range(2):
-            activate(g,384,512); gate(g,384,512)
-        store(0,384,512); store(1,384,512,'scalar')
+        multiply(uq, GATE_AT, 3)
+        for grp in range(G):
+            activate(grp, 3)
+            apply_gate(grp, 3)
+        store(0, 3)
+        store(1, 3, queue=nc.scalar)

@@ -25,12 +25,10 @@ LINE = 4
 MX_ALIGN = 64
 DMA_ALIGN = 256
 
-VECTOR_SHARE_FIRST = 160
-
 VECTOR_SHARE_TOGETHER = 72
 
-Z_AT = [[(0, 0), (2, 0), (3, 0), (1, 1)], [(0, 0), (0, 1), (2, 0), (0, 2)]]
-GATE_AT = [[(1, 0), (2, 1), (0, 1), (3, 1)], [(1, 0), (1, 1), (3, 0), (2, 1)]]
+Z_AT = [(0, 0), (2, 0), (3, 0), (1, 1)]
+GATE_AT = [(1, 0), (2, 1), (0, 1), (3, 1)]
 
 
 def tile_rows_gglu_tanh_kernel(tc, x, w, u, out):
@@ -75,7 +73,7 @@ def tile_rows_gglu_tanh_kernel(tc, x, w, u, out):
             return slice(STRIP * strip + HALF, STRIP * (strip + 1))
 
         def sums(place, grp, first, count=1):
-            bank, at = place[grp][first]
+            bank, at = place[first]
             return banks[grp][bank][:, strips(at, count)]
 
         def interleaving(op, cols):
@@ -87,11 +85,24 @@ def tile_rows_gglu_tanh_kernel(tc, x, w, u, out):
             dst, src = interleaving(op, cols)
             nc.vector.tensor_copy(out=dst, in_=src)
 
+        def pack_on_scalar(op, cols):
+            dst, src = interleaving(op, cols)
+            nc.scalar.copy(out=dst, in_=src)
+
+        def pack_on_gpsimd(op, cols):
+            nc.gpsimd.tensor_scalar(
+                out=op["packed"][:, cols, :],
+                in0=op["raw"][:, :, cols].rearrange("p j c -> p c j"),
+                scalar1=1.0,
+                scalar2=1.0,
+                op0=MULT,
+                op1=MULT,
+            )
+
         def pack(op, strip, vector_share):
             cut = STRIP * strip + vector_share
             pack_on_vector(op, slice(STRIP * strip, cut))
-            dst, src = interleaving(op, slice(cut, STRIP * (strip + 1)))
-            nc.scalar.copy(out=dst, in_=src)
+            pack_on_scalar(op, slice(cut, STRIP * (strip + 1)))
 
         def quantize(op, cols):
             nc.vector.quantize_mx(
@@ -130,57 +141,61 @@ def tile_rows_gglu_tanh_kernel(tc, x, w, u, out):
             cols = strips(first, count)
             queue.dma_start(out=out[grp, :, cols], in_=result[:, grp, cols])
 
+        def store_both(first, count=1, queue=nc.sync):
+            cols = strips(first, count)
+            queue.dma_start(out=out.rearrange("g m c -> m g c")[:, :, cols], in_=result[:, :, cols])
+
         def load_x(first, count=1):
             cols = strips(first, count)
             nc.sync.dma_start(out=x_raw[:, :, cols], in_=by_partition(x)[:, :, cols])
 
-        load_x(0, 2)
         nc.sync.dma_start(out=w_raw[:], in_=by_partition(w))
+        load_x(0)
         nc.sync.dma_start(out=u_raw[:], in_=by_partition(u))
-        load_x(2)
-        load_x(3)
+        for strip in range(1, N // STRIP):
+            load_x(strip)
 
-        pack_on_vector(xq, first_half(0))
-        pack_on_vector(xq, slice(HALF, VECTOR_SHARE_FIRST))
-        dst, src = interleaving(xq, slice(VECTOR_SHARE_FIRST, 2 * STRIP))
+        pack_on_vector(wq, first_half(0))
+        dst, src = interleaving(wq, second_half(0))
         nc.scalar.activation(out=dst, in_=src, func=COPY)
+
+        pack(xq, 0, HALF)
+        quantize(wq, strips(0))
         quantize(xq, first_half(0))
-
-        pack(wq, 0, VECTOR_SHARE_TOGETHER)
-        quantize(xq, second_half(0))
-        quantize(xq, strips(1))
-        quantize_halves(wq, 0)
-        multiply(wq, Z_AT, 0)
-        multiply(wq, Z_AT, 1)
-
         pack(uq, 0, HALF)
-        quantize_halves(uq, 0)
+        quantize(xq, second_half(0))
+        multiply(wq, Z_AT, 0)
+        quantize(uq, first_half(0))
+        pack(xq, 1, VECTOR_SHARE_TOGETHER)
+        quantize(uq, second_half(0))
         multiply(uq, GATE_AT, 0)
+        quantize_halves(xq, 1)
+        multiply(wq, Z_AT, 1)
         multiply(uq, GATE_AT, 1)
 
         pack(xq, 2, HALF)
         quantize_halves(xq, 2)
         activate(0, 0)
+        activate(1, 0)
         multiply(wq, Z_AT, 2)
         multiply(uq, GATE_AT, 2)
 
-        pack(xq, 3, VECTOR_SHARE_TOGETHER)
-        activate(1, 0, 2)
-        activate(0, 1)
+        pack_on_gpsimd(xq, first_half(3))
+        pack_on_scalar(xq, second_half(3))
         apply_gate(0, 0)
-        store(0, 0)
+        apply_gate(1, 0)
+        store_both(0)
         quantize_halves(xq, 3)
-        apply_gate(1, 0, 2)
-        store(1, 0, 2)
-        apply_gate(0, 1)
+        for grp in range(G):
+            activate(grp, 1)
+            apply_gate(grp, 1)
+        store_both(1)
 
         multiply(wq, Z_AT, 3)
-        activate(0, 2)
-        apply_gate(0, 2)
-        store(0, 1, 2)
-        activate(1, 2)
-        apply_gate(1, 2)
-        store(1, 2)
+        for grp in range(G):
+            activate(grp, 2)
+            apply_gate(grp, 2)
+        store_both(2)
 
         multiply(uq, GATE_AT, 3)
         for grp in range(G):

@@ -27,8 +27,8 @@ DMA_ALIGN = 256
 
 VECTOR_SHARE_TOGETHER = 72
 
-Z_AT = [(0, 0), (2, 0), (3, 0), (1, 1)]
-GATE_AT = [(1, 0), (2, 1), (0, 1), (3, 1)]
+Z_AT = [[(0, 0), (2, 0), (3, 0), (1, 1)], [(0, 0), (0, 1), (2, 0), (0, 2)]]
+GATE_AT = [[(1, 0), (2, 1), (0, 1), (3, 1)], [(1, 0), (1, 1), (3, 0), (2, 1)]]
 
 
 def tile_rows_gglu_tanh_kernel(tc, x, w, u, out):
@@ -73,7 +73,7 @@ def tile_rows_gglu_tanh_kernel(tc, x, w, u, out):
             return slice(STRIP * strip + HALF, STRIP * (strip + 1))
 
         def sums(place, grp, first, count=1):
-            bank, at = place[first]
+            bank, at = place[grp][first]
             return banks[grp][bank][:, strips(at, count)]
 
         def interleaving(op, cols):
@@ -85,24 +85,11 @@ def tile_rows_gglu_tanh_kernel(tc, x, w, u, out):
             dst, src = interleaving(op, cols)
             nc.vector.tensor_copy(out=dst, in_=src)
 
-        def pack_on_scalar(op, cols):
-            dst, src = interleaving(op, cols)
-            nc.scalar.copy(out=dst, in_=src)
-
-        def pack_on_gpsimd(op, cols):
-            nc.gpsimd.tensor_scalar(
-                out=op["packed"][:, cols, :],
-                in0=op["raw"][:, :, cols].rearrange("p j c -> p c j"),
-                scalar1=1.0,
-                scalar2=1.0,
-                op0=MULT,
-                op1=MULT,
-            )
-
         def pack(op, strip, vector_share):
             cut = STRIP * strip + vector_share
             pack_on_vector(op, slice(STRIP * strip, cut))
-            pack_on_scalar(op, slice(cut, STRIP * (strip + 1)))
+            dst, src = interleaving(op, slice(cut, STRIP * (strip + 1)))
+            nc.scalar.copy(out=dst, in_=src)
 
         def quantize(op, cols):
             nc.vector.quantize_mx(
@@ -141,9 +128,9 @@ def tile_rows_gglu_tanh_kernel(tc, x, w, u, out):
             cols = strips(first, count)
             queue.dma_start(out=out[grp, :, cols], in_=result[:, grp, cols])
 
-        def store_both(first, count=1, queue=nc.sync):
+        def store_both(first, count):
             cols = strips(first, count)
-            queue.dma_start(out=out.rearrange("g m c -> m g c")[:, :, cols], in_=result[:, :, cols])
+            nc.sync.dma_start(out=out.rearrange("g m c -> m g c")[:, :, cols], in_=result[:, :, cols])
 
         def load_x(first, count=1):
             cols = strips(first, count)
@@ -176,26 +163,25 @@ def tile_rows_gglu_tanh_kernel(tc, x, w, u, out):
         pack(xq, 2, HALF)
         quantize_halves(xq, 2)
         activate(0, 0)
-        activate(1, 0)
         multiply(wq, Z_AT, 2)
         multiply(uq, GATE_AT, 2)
 
-        pack_on_gpsimd(xq, first_half(3))
-        pack_on_scalar(xq, second_half(3))
+        pack(xq, 3, VECTOR_SHARE_TOGETHER)
+        activate(1, 0, 2)
+        activate(0, 1)
         apply_gate(0, 0)
-        apply_gate(1, 0)
-        store_both(0)
         quantize_halves(xq, 3)
-        for grp in range(G):
-            activate(grp, 1)
-            apply_gate(grp, 1)
-        store_both(1)
+        apply_gate(1, 0, 2)
+        apply_gate(0, 1)
+        store_both(0, 2)
 
         multiply(wq, Z_AT, 3)
-        for grp in range(G):
-            activate(grp, 2)
-            apply_gate(grp, 2)
-        store_both(2)
+        activate(0, 2)
+        apply_gate(0, 2)
+        store(0, 2)
+        activate(1, 2)
+        apply_gate(1, 2)
+        store(1, 2)
 
         multiply(uq, GATE_AT, 3)
         for grp in range(G):

@@ -26,6 +26,7 @@ MX_ALIGN = 64
 DMA_ALIGN = 256
 
 VECTOR_SHARE_TOGETHER = 72
+VECTOR_SHARE_FIRST = 160
 
 Z_AT = [[(0, 0), (2, 0), (3, 0), (1, 1)], [(0, 0), (0, 1), (2, 0), (0, 2)]]
 GATE_AT = [[(1, 0), (2, 1), (0, 1), (3, 1)], [(1, 0), (1, 1), (3, 0), (2, 1)]]
@@ -124,40 +125,36 @@ def tile_rows_gglu_tanh_kernel(tc, x, w, u, out):
                 out=result[:, grp, cols], in0=sums(GATE_AT, grp, first, count), in1=tanh_z[grp][:, cols], op=MULT
             )
 
-        def store(grp, first, count=1, queue=nc.sync):
+        def store_both(first, count, queue=nc.sync):
             cols = strips(first, count)
-            queue.dma_start(out=out[grp, :, cols], in_=result[:, grp, cols])
-
-        def store_both(first, count):
-            cols = strips(first, count)
-            nc.sync.dma_start(out=out.rearrange("g m c -> m g c")[:, :, cols], in_=result[:, :, cols])
+            queue.dma_start(out=out.rearrange("g m c -> m g c")[:, :, cols], in_=result[:, :, cols])
 
         def load_x(first, count=1):
             cols = strips(first, count)
             nc.sync.dma_start(out=x_raw[:, :, cols], in_=by_partition(x)[:, :, cols])
 
+        load_x(0, 2)
         nc.sync.dma_start(out=w_raw[:], in_=by_partition(w))
-        load_x(0)
         nc.sync.dma_start(out=u_raw[:], in_=by_partition(u))
-        for strip in range(1, N // STRIP):
+        for strip in range(2, N // STRIP):
             load_x(strip)
 
-        pack_on_vector(wq, first_half(0))
-        dst, src = interleaving(wq, second_half(0))
+        pack_on_vector(xq, first_half(0))
+        pack_on_vector(xq, slice(HALF, VECTOR_SHARE_FIRST))
+        dst, src = interleaving(xq, slice(VECTOR_SHARE_FIRST, 2 * STRIP))
         nc.scalar.activation(out=dst, in_=src, func=COPY)
-
-        pack(xq, 0, HALF)
-        quantize(wq, strips(0))
         quantize(xq, first_half(0))
-        pack(uq, 0, HALF)
+
+        pack(wq, 0, VECTOR_SHARE_TOGETHER)
         quantize(xq, second_half(0))
+        quantize(xq, strips(1))
+        quantize_halves(wq, 0)
         multiply(wq, Z_AT, 0)
-        quantize(uq, first_half(0))
-        pack(xq, 1, VECTOR_SHARE_TOGETHER)
-        quantize(uq, second_half(0))
-        multiply(uq, GATE_AT, 0)
-        quantize_halves(xq, 1)
         multiply(wq, Z_AT, 1)
+
+        pack(uq, 0, HALF)
+        quantize_halves(uq, 0)
+        multiply(uq, GATE_AT, 0)
         multiply(uq, GATE_AT, 1)
 
         pack(xq, 2, HALF)
@@ -176,16 +173,13 @@ def tile_rows_gglu_tanh_kernel(tc, x, w, u, out):
         store_both(0, 2)
 
         multiply(wq, Z_AT, 3)
-        activate(0, 2)
-        apply_gate(0, 2)
-        store(0, 2)
-        activate(1, 2)
-        apply_gate(1, 2)
-        store(1, 2)
+        for grp in range(G):
+            activate(grp, 2)
+            apply_gate(grp, 2)
+        store_both(2, 1)
 
         multiply(uq, GATE_AT, 3)
         for grp in range(G):
             activate(grp, 3)
             apply_gate(grp, 3)
-        store(0, 3)
-        store(1, 3, queue=nc.scalar)
+        store_both(3, 1, queue=nc.scalar)

@@ -125,9 +125,9 @@ def tile_rows_gglu_tanh_kernel(tc, x, w, u, out):
                 out=result[:, grp, cols], in0=sums(GATE_AT, grp, first, count), in1=tanh_z[grp][:, cols], op=MULT
             )
 
-        def store_both(first, count, queue=nc.sync):
+        def store_both(first, count):
             cols = strips(first, count)
-            queue.dma_start(out=out.rearrange("g m c -> m g c")[:, :, cols], in_=result[:, :, cols])
+            nc.sync.dma_start(out=out.rearrange("g m c -> m g c")[:, :, cols], in_=result[:, :, cols])
 
         def load_x(first, count=1):
             cols = strips(first, count)
@@ -182,4 +182,4 @@ def tile_rows_gglu_tanh_kernel(tc, x, w, u, out):
         for grp in range(G):
             activate(grp, 3)
             apply_gate(grp, 3)
-        store_both(3, 1, queue=nc.scalar)
+        store_both(3, 1)

@@ -28,8 +28,8 @@ DMA_ALIGN = 256
 VECTOR_SHARE_TOGETHER = 72
 VECTOR_SHARE_FIRST = 160
 
-Z_AT = [[(0, 0), (2, 0), (3, 0), (1, 1)], [(0, 0), (0, 1), (2, 0), (0, 2)]]
-GATE_AT = [[(1, 0), (2, 1), (0, 1), (3, 1)], [(1, 0), (1, 1), (3, 0), (2, 1)]]
+Z_AT = [[(0, 0), (2, 0), (3, 0), (1, 1)], [(0, 0), (2, 0), (3, 0), (2, 1)]]
+GATE_AT = [[(1, 0), (2, 1), (0, 1), (3, 1)], [(1, 0), (1, 1), (0, 1), (3, 1)]]
 
 
 def tile_rows_gglu_tanh_kernel(tc, x, w, u, out):
@@ -160,11 +160,12 @@ def tile_rows_gglu_tanh_kernel(tc, x, w, u, out):
         pack(xq, 2, HALF)
         quantize_halves(xq, 2)
         activate(0, 0)
+        activate(1, 0)
         multiply(wq, Z_AT, 2)
         multiply(uq, GATE_AT, 2)
 
         pack(xq, 3, VECTOR_SHARE_TOGETHER)
-        activate(1, 0, 2)
+        activate(1, 1)
         activate(0, 1)
         apply_gate(0, 0)
         quantize_halves(xq, 3)

@@ -21,7 +21,7 @@ STRIP = 128
 HALF = STRIP // 2
 BANK = 512
 BANKS_PER_GROUP = 4
-LINE = 4
+LINE = 2
 MX_ALIGN = 64
 DMA_ALIGN = 256
 

@@ -24,9 +24,7 @@ BANKS_PER_GROUP = 4
 LINE = 2
 MX_ALIGN = 64
 DMA_ALIGN = 256
-
-VECTOR_SHARE_TOGETHER = 72
-VECTOR_SHARE_FIRST = 160
+STAGGER = 256
 
 Z_AT = [[(0, 0), (2, 0), (3, 0), (1, 1)], [(0, 0), (2, 0), (3, 0), (2, 1)]]
 GATE_AT = [[(1, 0), (2, 1), (0, 1), (3, 1)], [(1, 0), (1, 1), (0, 1), (3, 1)]]
@@ -43,78 +41,73 @@ def tile_rows_gglu_tanh_kernel(tc, x, w, u, out):
         ps = ctx.enter_context(tc.psum_pool(name="ps", bufs=1))
         ctx.enter_context(tc.manual_schedule())
 
-        w_raw = sb.tile([P, PACK, M], F32, name="w_raw", align_bytes=DMA_ALIGN)
-        u_raw = sb.tile([P, PACK, M], F32, name="u_raw", align_bytes=DMA_ALIGN)
-        x_raw = sb.tile([P, PACK, N], F32, name="x_raw", align_bytes=DMA_ALIGN)
-
-        def operand(name, raw, width):
+        def operand(name, width, codes_at, scales_at):
+            count = width // STRIP
+            codes = sb.tile([P, width + STAGGER // 4], U32, name=name + "_codes", align_bytes=STAGGER)
+            scales = sb.tile([P, count, 2 * STAGGER], U8, name=name + "_scales", align_bytes=STAGGER)
             return {
-                "raw": raw,
+                "raw": sb.tile([P, PACK, width], F32, name=name + "_raw", align_bytes=DMA_ALIGN),
                 "packed": sb.tile([P, width, PACK], BF16, name=name + "_packed", align_bytes=MX_ALIGN),
-                "codes": sb.tile([P, width], U32, name=name + "_codes", align_bytes=MX_ALIGN),
-                "scales": sb.tile([P, width], U8, name=name + "_scales", align_bytes=MX_ALIGN),
+                "codes": codes[:, codes_at // 4 : codes_at // 4 + width],
+                "scales": scales[:, :, scales_at : scales_at + STRIP],
             }
 
-        wq = operand("w", w_raw, M)
-        uq = operand("u", u_raw, M)
-        xq = operand("x", x_raw, N)
+        def scales_of(op, rows, lo, hi):
+            strip = lo // STRIP
+            return op["scales"][rows, strip, lo - STRIP * strip : hi - STRIP * strip]
+
+        wq = operand("w", M, 0, 64)
+        uq = operand("u", M, 0, 64)
+        xq = operand("x", N, 128, 192)
         banks = [
             [ps.tile([P, BANK], F32, name="bank%d_%d" % (grp, b)) for b in range(BANKS_PER_GROUP)] for grp in range(G)
         ]
         tanh_z = [sb.tile([P, N], F32, name="tanh_z%d" % grp) for grp in range(G)]
         result = sb.tile([P, G, N], F32, name="result", align_bytes=DMA_ALIGN)
+        out_rows = out.rearrange("g m c -> m g c")
 
         def strips(first, count=1):
             return slice(STRIP * first, STRIP * (first + count))
-
-        def first_half(strip):
-            return slice(STRIP * strip, STRIP * strip + HALF)
-
-        def second_half(strip):
-            return slice(STRIP * strip + HALF, STRIP * (strip + 1))
 
         def sums(place, grp, first, count=1):
             bank, at = place[grp][first]
             return banks[grp][bank][:, strips(at, count)]
 
-        def interleaving(op, cols):
-            dst = op["packed"][:, cols, :].rearrange("p (c i) j -> p c j i", i=LINE)
-            src = op["raw"][:, :, cols].rearrange("p j (c i) -> p c j i", i=LINE)
+        def interleaving(op, lo, hi):
+            dst = op["packed"][:, lo:hi, :].rearrange("p (c i) j -> p c j i", i=LINE)
+            src = op["raw"][:, :, lo:hi].rearrange("p j (c i) -> p c j i", i=LINE)
             return dst, src
 
-        def pack_on_vector(op, cols):
-            dst, src = interleaving(op, cols)
+        def pack_vector(op, lo, hi):
+            dst, src = interleaving(op, lo, hi)
             nc.vector.tensor_copy(out=dst, in_=src)
 
-        def pack(op, strip, vector_share):
-            cut = STRIP * strip + vector_share
-            pack_on_vector(op, slice(STRIP * strip, cut))
-            dst, src = interleaving(op, slice(cut, STRIP * (strip + 1)))
+        def pack_scalar(op, lo, hi):
+            dst, src = interleaving(op, lo, hi)
             nc.scalar.copy(out=dst, in_=src)
 
-        def quantize(op, cols):
+        def quantize(op, lo, hi):
             nc.vector.quantize_mx(
-                out=op["codes"][:, cols].bitcast(FP8X4),
-                scales=op["scales"][:, cols],
-                in_=op["packed"][:, cols, :].rearrange("p c j -> p (c j)"),
+                out=op["codes"][:, lo:hi].bitcast(FP8X4),
+                scales=scales_of(op, slice(0, P), lo, hi),
+                in_=op["packed"][:, lo:hi, :].rearrange("p c j -> p (c j)"),
             )
 
-        def quantize_halves(op, strip):
-            quantize(op, first_half(strip))
-            quantize(op, second_half(strip))
+        def one_pass(weights, place, grp, strip):
+            rows = slice(ROWS * grp, ROWS * (grp + 1))
+            nc.tensor.matmul_mx(
+                out=sums(place, grp, strip),
+                lhsT=weights["codes"][rows, :].bitcast(FP8X4),
+                lhsT_scale=scales_of(weights, rows, 0, M),
+                rhs=xq["codes"][rows, strips(strip)].bitcast(FP8X4),
+                rhs_scale=scales_of(xq, rows, STRIP * strip, STRIP * (strip + 1)),
+                start=True,
+                stop=True,
+            )
 
         def multiply(weights, place, strip):
             for grp in range(G):
-                rows = slice(ROWS * grp, ROWS * (grp + 1))
-                nc.tensor.matmul_mx(
-                    out=sums(place, grp, strip),
-                    lhsT=weights["codes"][rows, :].bitcast(FP8X4),
-                    lhsT_scale=weights["scales"][rows, :],
-                    rhs=xq["codes"][rows, strips(strip)].bitcast(FP8X4),
-                    rhs_scale=xq["scales"][rows, strips(strip)],
-                    start=True,
-                    stop=True,
-                )
+                one_pass(weights, place, grp, strip)
 
         def activate(grp, first, count=1):
             nc.scalar.activation(out=tanh_z[grp][:, strips(first, count)], in_=sums(Z_AT, grp, first, count), func=TANH)
@@ -125,62 +118,70 @@ def tile_rows_gglu_tanh_kernel(tc, x, w, u, out):
                 out=result[:, grp, cols], in0=sums(GATE_AT, grp, first, count), in1=tanh_z[grp][:, cols], op=MULT
             )
 
-        def store_both(first, count):
+        def store(queue, groups, first, count):
             cols = strips(first, count)
-            nc.sync.dma_start(out=out.rearrange("g m c -> m g c")[:, :, cols], in_=result[:, :, cols])
+            queue.dma_start(out=out_rows[:, groups, cols], in_=result[:, groups, cols])
 
-        def load_x(first, count=1):
-            cols = strips(first, count)
-            nc.sync.dma_start(out=x_raw[:, :, cols], in_=by_partition(x)[:, :, cols])
+        def load(op, source, lo, hi):
+            nc.sync.dma_start(out=op["raw"][:, :, lo:hi], in_=by_partition(source)[:, :, lo:hi])
 
-        load_x(0, 2)
-        nc.sync.dma_start(out=w_raw[:], in_=by_partition(w))
-        nc.sync.dma_start(out=u_raw[:], in_=by_partition(u))
-        for strip in range(2, N // STRIP):
-            load_x(strip)
+        both = slice(0, G)
+        load(xq, x, 0, 256)
+        load(wq, w, 0, M)
+        load(uq, u, 0, M)
+        load(xq, x, 256, 384)
+        load(xq, x, 384, 512)
 
-        pack_on_vector(xq, first_half(0))
-        pack_on_vector(xq, slice(HALF, VECTOR_SHARE_FIRST))
-        dst, src = interleaving(xq, slice(VECTOR_SHARE_FIRST, 2 * STRIP))
+        pack_vector(xq, 0, 64)
+        pack_vector(xq, 64, 160)
+        dst, src = interleaving(xq, 160, 256)
         nc.scalar.activation(out=dst, in_=src, func=COPY)
-        quantize(xq, first_half(0))
+        quantize(xq, 0, 64)
 
-        pack(wq, 0, VECTOR_SHARE_TOGETHER)
-        quantize(xq, second_half(0))
-        quantize(xq, strips(1))
-        quantize_halves(wq, 0)
+        pack_vector(wq, 0, 72)
+        pack_scalar(wq, 72, M)
+        quantize(xq, 64, 128)
+        quantize(xq, 128, 256)
+        quantize(wq, 0, HALF)
+        quantize(wq, HALF, M)
         multiply(wq, Z_AT, 0)
         multiply(wq, Z_AT, 1)
 
-        pack(uq, 0, HALF)
-        quantize_halves(uq, 0)
+        pack_vector(uq, 0, 64)
+        pack_scalar(uq, 64, M)
+        quantize(uq, 0, HALF)
+        quantize(uq, HALF, M)
         multiply(uq, GATE_AT, 0)
         multiply(uq, GATE_AT, 1)
 
-        pack(xq, 2, HALF)
-        quantize_halves(xq, 2)
+        pack_vector(xq, 256, 320)
+        pack_scalar(xq, 320, 384)
+        quantize(xq, 256, 320)
+        quantize(xq, 320, 384)
         activate(0, 0)
         activate(1, 0)
         multiply(wq, Z_AT, 2)
         multiply(uq, GATE_AT, 2)
 
-        pack(xq, 3, VECTOR_SHARE_TOGETHER)
+        pack_vector(xq, 384, 456)
+        pack_scalar(xq, 456, 512)
         activate(1, 1)
         activate(0, 1)
         apply_gate(0, 0)
-        quantize_halves(xq, 3)
+        quantize(xq, 384, 448)
+        quantize(xq, 448, 512)
         apply_gate(1, 0, 2)
         apply_gate(0, 1)
-        store_both(0, 2)
+        store(nc.sync, both, 0, 2)
 
         multiply(wq, Z_AT, 3)
         for grp in range(G):
             activate(grp, 2)
             apply_gate(grp, 2)
-        store_both(2, 1)
+        store(nc.sync, both, 2, 1)
 
         multiply(uq, GATE_AT, 3)
         for grp in range(G):
             activate(grp, 3)
             apply_gate(grp, 3)
-        store_both(3, 1)
+        store(nc.sync, both, 3, 1)

@@ -25,6 +25,7 @@ LINE = 2
 MX_ALIGN = 64
 DMA_ALIGN = 256
 STAGGER = 256
+STORES = [(0, 2), (2, 1), (3, 1)]
 
 Z_AT = [[(0, 0), (2, 0), (3, 0), (1, 1)], [(0, 0), (2, 0), (3, 0), (2, 1)]]
 GATE_AT = [[(1, 0), (2, 1), (0, 1), (3, 1)], [(1, 0), (1, 1), (0, 1), (3, 1)]]
@@ -63,7 +64,10 @@ def tile_rows_gglu_tanh_kernel(tc, x, w, u, out):
             [ps.tile([P, BANK], F32, name="bank%d_%d" % (grp, b)) for b in range(BANKS_PER_GROUP)] for grp in range(G)
         ]
         tanh_z = [sb.tile([P, N], F32, name="tanh_z%d" % grp) for grp in range(G)]
-        result = sb.tile([P, G, N], F32, name="result", align_bytes=DMA_ALIGN)
+        results = {
+            first: sb.tile([P, G, STRIP * count], F32, name="result%d" % first, align_bytes=DMA_ALIGN)
+            for first, count in STORES
+        }
         out_rows = out.rearrange("g m c -> m g c")
 
         def strips(first, count=1):
@@ -112,15 +116,19 @@ def tile_rows_gglu_tanh_kernel(tc, x, w, u, out):
         def activate(grp, first, count=1):
             nc.scalar.activation(out=tanh_z[grp][:, strips(first, count)], in_=sums(Z_AT, grp, first, count), func=TANH)
 
+        def result_of(grp, first, count):
+            base = max(at for at, width in STORES if at <= first)
+            return results[base][:, grp, strips(first - base, count)]
+
         def apply_gate(grp, first, count=1):
             cols = strips(first, count)
             nc.vector.tensor_tensor(
-                out=result[:, grp, cols], in0=sums(GATE_AT, grp, first, count), in1=tanh_z[grp][:, cols], op=MULT
+                out=result_of(grp, first, count), in0=sums(GATE_AT, grp, first, count), in1=tanh_z[grp][:, cols], op=MULT
             )
 
         def store(queue, groups, first, count):
             cols = strips(first, count)
-            queue.dma_start(out=out_rows[:, groups, cols], in_=result[:, groups, cols])
+            queue.dma_start(out=out_rows[:, groups, cols], in_=results[first][:, groups, :])
 
         def load(op, source, lo, hi):
             nc.sync.dma_start(out=op["raw"][:, :, lo:hi], in_=by_partition(source)[:, :, lo:hi])

from contextlib import ExitStack

import concourse.mybir as mybir

G, D, M, N = 2, 256, 128, 512
FLOPS = 2 * 2 * G * D * M * N

F32 = mybir.dt.float32
BF16 = mybir.dt.bfloat16
U32 = mybir.dt.uint32
U8 = mybir.dt.uint8
FP8X4 = mybir.dt.float8_e4m3fn_x4
TANH = mybir.ActivationFunctionType.Tanh
COPY = mybir.ActivationFunctionType.Copy
MULT = mybir.AluOpType.mult

P = 128
PACK = 4
ROWS = D // PACK
STRIP = 128
HALF = STRIP // 2
BANK = 512
BANKS_PER_GROUP = 4
LINE = 2
MX_ALIGN = 64
DMA_ALIGN = 256
STAGGER = 256
STORES = [(0, 2), (2, 1), (3, 1)]

Z_AT = [[(0, 0), (2, 0), (3, 0), (1, 1)], [(0, 0), (2, 0), (3, 0), (2, 1)]]
GATE_AT = [[(1, 0), (2, 1), (0, 1), (3, 1)], [(1, 0), (1, 1), (0, 1), (3, 1)]]


def tile_rows_gglu_tanh_kernel(tc, x, w, u, out):
    nc = tc.nc

    def by_partition(t):
        return t.rearrange("g d c -> (g d) c").rearrange("(p j) c -> p j c", j=PACK)

    with ExitStack() as ctx:
        sb = ctx.enter_context(tc.tile_pool(name="sb", bufs=1))
        ps = ctx.enter_context(tc.psum_pool(name="ps", bufs=1))
        ctx.enter_context(tc.manual_schedule())

        def operand(name, width, codes_at, scales_at):
            count = width // STRIP
            codes = sb.tile([P, width + STAGGER // 4], U32, name=name + "_codes", align_bytes=STAGGER)
            scales = sb.tile([P, count, 2 * STAGGER], U8, name=name + "_scales", align_bytes=STAGGER)
            return {
                "raw": sb.tile([P, PACK, width], F32, name=name + "_raw", align_bytes=DMA_ALIGN),
                "packed": sb.tile([P, width, PACK], BF16, name=name + "_packed", align_bytes=MX_ALIGN),
                "codes": codes[:, codes_at // 4 : codes_at // 4 + width],
                "scales": scales[:, :, scales_at : scales_at + STRIP],
            }

        def scales_of(op, rows, lo, hi):
            strip = lo // STRIP
            return op["scales"][rows, strip, lo - STRIP * strip : hi - STRIP * strip]

        wq = operand("w", M, 0, 64)
        uq = operand("u", M, 0, 64)
        xq = operand("x", N, 128, 192)
        banks = [
            [ps.tile([P, BANK], F32, name="bank%d_%d" % (grp, b)) for b in range(BANKS_PER_GROUP)] for grp in range(G)
        ]
        tanh_z = [sb.tile([P, N], F32, name="tanh_z%d" % grp) for grp in range(G)]
        results = {
            first: sb.tile([P, G, STRIP * count], F32, name="result%d" % first, align_bytes=DMA_ALIGN)
            for first, count in STORES
        }
        out_rows = out.rearrange("g m c -> m g c")

        def strips(first, count=1):
            return slice(STRIP * first, STRIP * (first + count))

        def sums(place, grp, first, count=1):
            bank, at = place[grp][first]
            return banks[grp][bank][:, strips(at, count)]

        def interleaving(op, lo, hi):
            dst = op["packed"][:, lo:hi, :].rearrange("p (c i) j -> p c j i", i=LINE)
            src = op["raw"][:, :, lo:hi].rearrange("p j (c i) -> p c j i", i=LINE)
            return dst, src

        def pack_vector(op, lo, hi):
            dst, src = interleaving(op, lo, hi)
            nc.vector.tensor_copy(out=dst, in_=src)

        def pack_scalar(op, lo, hi):
            dst, src = interleaving(op, lo, hi)
            nc.scalar.copy(out=dst, in_=src)

        def quantize(op, lo, hi):
            nc.vector.quantize_mx(
                out=op["codes"][:, lo:hi].bitcast(FP8X4),
                scales=scales_of(op, slice(0, P), lo, hi),
                in_=op["packed"][:, lo:hi, :].rearrange("p c j -> p (c j)"),
            )

        def one_pass(weights, place, grp, strip):
            rows = slice(ROWS * grp, ROWS * (grp + 1))
            nc.tensor.matmul_mx(
                out=sums(place, grp, strip),
                lhsT=weights["codes"][rows, :].bitcast(FP8X4),
                lhsT_scale=scales_of(weights, rows, 0, M),
                rhs=xq["codes"][rows, strips(strip)].bitcast(FP8X4),
                rhs_scale=scales_of(xq, rows, STRIP * strip, STRIP * (strip + 1)),
                start=True,
                stop=True,
            )

        def multiply(weights, place, strip):
            for grp in range(G):
                one_pass(weights, place, grp, strip)

        def activate(grp, first, count=1):
            nc.scalar.activation(out=tanh_z[grp][:, strips(first, count)], in_=sums(Z_AT, grp, first, count), func=TANH)

        def result_of(grp, first, count):
            base = max(at for at, width in STORES if at <= first)
            return results[base][:, grp, strips(first - base, count)]

        def apply_gate(grp, first, count=1):
            cols = strips(first, count)
            nc.vector.tensor_tensor(
                out=result_of(grp, first, count), in0=sums(GATE_AT, grp, first, count), in1=tanh_z[grp][:, cols], op=MULT
            )

        def store(queue, groups, first, count):
            cols = strips(first, count)
            queue.dma_start(out=out_rows[:, groups, cols], in_=results[first][:, groups, :])

        def load(op, source, lo, hi):
            nc.sync.dma_start(out=op["raw"][:, :, lo:hi], in_=by_partition(source)[:, :, lo:hi])

        both = slice(0, G)
        load(xq, x, 0, 256)
        load(wq, w, 0, M)
        load(uq, u, 0, M)
        load(xq, x, 256, 384)
        load(xq, x, 384, 512)

        pack_vector(xq, 0, 64)
        pack_vector(xq, 64, 160)
        dst, src = interleaving(xq, 160, 256)
        nc.scalar.activation(out=dst, in_=src, func=COPY)
        quantize(xq, 0, 64)

        pack_vector(wq, 0, 72)
        pack_scalar(wq, 72, M)
        quantize(xq, 64, 128)
        quantize(xq, 128, 256)
        quantize(wq, 0, HALF)
        quantize(wq, HALF, M)
        multiply(wq, Z_AT, 0)
        multiply(wq, Z_AT, 1)

        pack_vector(uq, 0, 64)
        pack_scalar(uq, 64, M)
        quantize(uq, 0, HALF)
        quantize(uq, HALF, M)
        multiply(uq, GATE_AT, 0)
        multiply(uq, GATE_AT, 1)

        pack_vector(xq, 256, 320)
        pack_scalar(xq, 320, 384)
        quantize(xq, 256, 320)
        quantize(xq, 320, 384)
        activate(0, 0)
        activate(1, 0)
        multiply(wq, Z_AT, 2)
        multiply(uq, GATE_AT, 2)

        pack_vector(xq, 384, 456)
        pack_scalar(xq, 456, 512)
        activate(1, 1)
        activate(0, 1)
        apply_gate(0, 0)
        quantize(xq, 384, 448)
        quantize(xq, 448, 512)
        apply_gate(1, 0, 2)
        apply_gate(0, 1)
        store(nc.sync, both, 0, 2)

        multiply(wq, Z_AT, 3)
        for grp in range(G):
            activate(grp, 2)
            apply_gate(grp, 2)
        store(nc.sync, both, 2, 1)

        multiply(uq, GATE_AT, 3)
        for grp in range(G):
            activate(grp, 3)
            apply_gate(grp, 3)
        store(nc.sync, both, 3, 1)
